import numpy as np, ml_dtypes
CORES = [40,41,42,43,44,45,46,47]
N = 8
BF = ml_dtypes.bfloat16
S, M, CAP, L = 512, 512, 112, 6
F = 16 // N
def tries(rng, same=False, few=False):
    kid = np.zeros((N, 8, M, 16), np.int32); words = {}; deep = {}
    tid = (rng.integers(1, 65536, (N, 8, M)) * (rng.random((N, 8, M)) < (0.0625 if few else 0.5))).astype(np.int32)
    for q in range(N):
        for g in range(8):
            no = [0, 1] + (2 + rng.permutation(M - 2)).tolist(); pl = rng.random(M).tolist(); cl = rng.integers(0, 16, M).tolist()
            k = kid[q, g]; w = {1: []}; up = []; m = 2; deep[q, g] = []
            for c in (q * F + rng.permutation(F)).tolist()[:1 if few else F]:
                p = 1
                for d in range(L):
                    e = c if d == 0 or same else cl[m]
                    k[no[p], e] = no[m]; w[m] = w[p] + [e]
                    if d < L - 1: up.append(m)
                    p = m; m += 1
                tid[q, g, no[p]] = rng.integers(1, 65536); deep[q, g].append(w[p])
            for m in range(m, M):
                p = up[int(pl[m] * len(up))]; e = cl[m]
                if k[no[p], e]: continue
                k[no[p], e] = no[m]; w[m] = w[p] + [e]
                if len(w[m]) < L: up.append(m)
            words[q, g] = [v for v in w.values() if v]
    tid[:, :, 0] = 0
    return kid.reshape(N, 8, 16 * M), tid, words, deep
def strings(rng, words):
    s = np.zeros((8, N * S), np.int64)
    for g in range(8):
        qs = rng.integers(0, N, N * S).tolist(); ms = rng.random(N * S).tolist(); a = []; i = 0
        while len(a) < N * S:
            v = words[qs[i], g]; a += v[int(ms[i] * len(v))]; i += 1
        s[g] = a[:N * S]
    return np.where(rng.random(s.shape) < 0.1, rng.integers(0, 16, s.shape), s)
def plant(rng, s, deep):
    keep = np.zeros(s.shape, bool)
    for r in range(N):
        for g in range(8):
            v = deep[int(rng.integers(0, N)), g]; j = (r * S + S - 1 - g % (L - 1) + np.arange(L)) % (N * S)
            s[g, j] = v[int(rng.integers(0, len(v)))]; keep[g, j] = True
    return keep
def fit(rng, s, keep, full=False):
    s = s.reshape(8, N, S).transpose(1, 0, 2).astype(np.int32); keep = keep.reshape(8, N, S).transpose(1, 0, 2)
    a, b = int(rng.integers(0, N)), int(rng.integers(0, 8))
    for r in range(N):
        for g in range(8):
            e = s[r, g]; own = e // F; have = np.bincount(own, minlength=N); low = np.bincount(own[keep[r, g]], minlength=N)
            o = rng.permutation(N); i = np.flatnonzero((o == a) if full and g == b else (o != r))[0]; o[[0, i]] = o[[i, 0]]
            want = low.copy() if full else np.minimum(have, CAP)
            if full or (r, g) == (a, b): want[o[0]] = CAP
            for q in np.roll(o, -1): want[q] = min(max(int(want[q]) + S - int(np.sum(want)), int(low[q])), CAP)
            sur = np.concatenate([rng.permutation(np.flatnonzero((own == q) & ~keep[r, g]))[:max(int(have[q] - want[q]), 0)] for q in range(N)])
            need = np.repeat(np.arange(N), np.maximum(want - have, 0))
            e[sur] = need * F + rng.integers(0, F, len(need))
    return np.ascontiguousarray(s)
def setup_inputs(rng):
    kid, tid, words, deep = tries(rng); s = strings(rng, words); keep = plant(rng, s, deep)
    return {"lett": fit(rng, s, keep), "kid": kid, "tid": tid}
def setup_inputs_full(rng):
    kid, tid, words, deep = tries(rng); s = strings(rng, words)
    lett = fit(rng, s, np.zeros(s.shape, bool), True)
    assert np.sum((lett // F)[..., None] == np.arange(N), axis=2).min(axis=0).max() == CAP
    return {"lett": lett, "kid": kid, "tid": tid}
def setup_inputs_runs(rng):
    kid, tid, words, deep = tries(rng, same=True)
    s = np.stack([np.repeat(rng.integers(0, 16, N * S), rng.integers(1, 13, N * S))[:N * S] for g in range(8)]); keep = plant(rng, s, deep)
    return {"lett": fit(rng, s, keep), "kid": kid, "tid": tid}
def setup_inputs_few(rng):
    kid, tid, words, deep = tries(rng, few=True); s = strings(rng, words); keep = plant(rng, s, deep)
    return {"lett": fit(rng, s, keep), "kid": kid, "tid": tid}
def setup_inputs_spread(rng):
    kid = (rng.integers(0, M, (N, 8, M, 16)) * (rng.random((N, 8, M, 16)) > 0.125)).astype(np.int32)
    kid[:, :, 0] = 0; kid[:, :, 1] *= (np.arange(16) // F == np.arange(N)[:, None])[:, None, :]
    tid = (rng.integers(0, 65536, (N, 8, M)) * (rng.random((N, 8, M)) < 0.3)).astype(np.int32); tid[:, :, 0] = 0; tid[:, :, M - 1] = 65535
    s = np.minimum(np.floor(rng.random((8, N * S)) ** 2 * 16), 15).astype(np.int64)
    return {"lett": fit(rng, s, np.zeros(s.shape, bool)), "kid": kid.reshape(N, 8, 16 * M), "tid": tid}
def check_inputs(d):
    bad = []; s, kid, tid = d["lett"], d["kid"], d["tid"]
    if s.min() < 0 or s.max() > 15: bad.append("letters")
    if ((s // F)[..., None] == np.arange(N)).sum(2).max() > CAP: bad.append("slots")
    if kid.min() < 0 or kid.max() >= M: bad.append("children")
    if kid[:, :, :16].any() or tid[:, :, 0].any(): bad.append("node 0")
    if (kid[:, :, 16:32] * (np.arange(16) // F != np.arange(N)[:, None])[:, None, :]).any(): bad.append("roots")
    if tid.min() < 0 or tid.max() > 65535: bad.append("ids")
    return bad
def reference(lett, kid, tid):
    s = np.concatenate(list(lett), axis=1).astype(np.int64)
    own = s // F; g = np.arange(8)[:, None]; node = np.ones(s.shape, np.int64); yl = np.zeros(s.shape, np.int64); yi = np.zeros(s.shape, np.int64)
    for k in range(L):
        node = kid[own, g, 16 * node + np.roll(s, -k, axis=1)].astype(np.int64)
        t = tid[own, g, node]
        yl = np.where(t > 0, k + 1, yl); yi = np.where(t > 0, t, yi)
    yl = np.ascontiguousarray(yl.reshape(8, N, S).transpose(1, 0, 2)); yi = np.ascontiguousarray(yi.reshape(8, N, S).transpose(1, 0, 2))
    return {"ylen": yl.astype(np.float32), "yid": yi.astype(np.float32)}

@@ -1,0 +1,314 @@
+from concourse.bass import DstId, RemoteDMATransfer
+from concourse.mybir import AluOpType as A, ActivationFunctionType as F
+
+N = 8
+SCRATCH = {
+    "kraw": ("sbuf", [128, 32, 16], "int32"),
+    "kb": ("sbuf", [128, 4, 128], "bfloat16"),
+    "win": ("sbuf", [128, 4096], "bfloat16"),
+    "idwin": ("sbuf", [128, 4096], "bfloat16"),
+    "wl": ("sbuf", [128, 32], "int32"),
+    "wlb": ("sbuf", [128, 32], "bfloat16"),
+    "halo": ("sbuf", [128, 8], "int32"),
+    "halob": ("sbuf", [128, 8], "bfloat16"),
+    "wq": ("sbuf", [128, 32], "int32"),
+    "tidr": ("sbuf", [128, 32], "int32"),
+    "ta": ("sbuf", [128, 32], "int32"),
+    "tz": ("sbuf", [128, 32], "int32"),
+    "tl": ("sbuf", [128, 32], "int32"),
+    "idhi": ("sbuf", [128, 32], "bfloat16"),
+    "idlo": ("sbuf", [128, 32], "bfloat16"),
+    "rrow": ("sbuf", [128, 256], "int32"),
+    "rf": ("sbuf", [128, 128], "float32"),
+    "onesf": ("sbuf", [128, 1], "float32"),
+    "rcol": ("sbuf", [128, 1], "float32"),
+    "ones": ("sbuf", [128, 128], "bfloat16"),
+    "blk1": ("sbuf", [128, 128], "bfloat16"),
+    "blk": ("sbuf", [128, 128], "bfloat16"),
+    "ident": ("sbuf", [128, 128], "bfloat16"),
+    "wr": ("sbuf", [128, 4, 128], "bfloat16"),
+    "pick": ("sbuf", [128, 16, 128], "bfloat16"),
+    "iop": ("sbuf", [128, 1], "int32"),
+    "iof": ("sbuf", [128, 16], "float32"),
+    "ri": ("sbuf", [128, 1], "int32"),
+    "rr": ("sbuf", [128, 1], "float32"),
+    "wsi": ("sbuf", [128, 1], "int32"),
+    "ws": ("sbuf", [128, 1], "float32"),
+    "rm": ("sbuf", [128, 16], "float32"),
+    "eq": ("sbuf", [128, 8], "float32"),
+    "dd": ("sbuf", [128, 4], "float32"),
+    "d1": ("sbuf", [128, 4], "float32"),
+    "d2": ("sbuf", [128, 4], "float32"),
+    "c3": ("sbuf", [128, 1], "float32"),
+    "c4": ("sbuf", [128, 1], "float32"),
+    "bc": ("sbuf", [128, 1], "float32"),
+    "bk": ("sbuf", [128, 6], "float32"),
+    "zer": ("sbuf", [128, 32], "float32"),
+    "dk": ("sbuf", [128, 128], "float32"),
+    "dy": ("sbuf", [128, 128], "float32"),
+    "em": ("sbuf", [128, 592], "bfloat16"),
+    "x0": ("sbuf", [128, 256], "bfloat16"),
+    "x1": ("sbuf", [128, 256], "bfloat16"),
+    "sc0": ("sbuf", [128, 64], "float32"),
+    "sc1": ("sbuf", [128, 64], "float32"),
+    "scy": ("sbuf", [128, 128], "float32"),
+    "acc": ("sbuf", [128, 128], "float32"),
+    "keyi": ("sbuf", [128, 32], "int32"),
+    "leni": ("sbuf", [128, 32], "int32"),
+    "idi": ("sbuf", [128, 32], "int32"),
+    "yl": ("sbuf", [128, 32], "float32"),
+    "yi": ("sbuf", [128, 32], "float32"),
+    "rl": ("dram", [8, 128, 2], "int32"),
+    "idl": ("dram", [8, 128, 64], "bfloat16"),
+}
+for _k in range(1, 7):
+    SCRATCH["l%d" % _k] = ("sbuf", [128, 32], "uint16")
+for _k in range(4):
+    SCRATCH["y%d" % _k] = ("sbuf", [128, 256], "bfloat16")
+for _k in range(7):
+    SCRATCH["p%d" % _k] = ("psum", [128, 512], "float32")
+SEMAPHORES = ["cv", "cs", "ct", "cg", "dl", "dr", "dt", "dhi", "dlo", "drr", "didw", "dyl", "dyi",
+              "halo_in", "r_in", "id_in", "k_in", "halo_out", "r_out", "id_out", "k_out"] + ["dk%d" % k for k in range(8)]
+
+
+def rank_program(g, core, T, topo):
+    me = T.rank_of(core)
+    if me is None:
+        return
+    q = {"v": g.vector, "s": g.scalar, "t": g.tensor, "g": g, "y": g.sync}
+    total, seen = {}, {k: {} for k in q}
+
+    def wait(k, *toks):
+        for tok in toks:
+            if tok is not None and seen[k].get(tok[0], 0) < tok[1]:
+                q[k].wait_ge(T.sem[tok[0]], tok[1])
+                seen[k][tok[0]] = tok[1]
+
+    def done(sem, inst, n=1):
+        inst.then_inc(T.sem[sem], n)
+        total[sem] = total.get(sem, 0) + n
+        return (sem, total[sem])
+
+    def V(inst): return done("cv", inst)
+    def S(inst): return done("cs", inst)
+    def P(inst): return done("ct", inst)
+    def G(inst): return done("cg", inst)
+    v, s, t, sy = g.vector, g.scalar, g.tensor, g.sync
+    peers = [T.cores[(me + d) % N] for d in range(1, N)]
+    mask = topo.mask(core, peers[0])
+    for c in peers:
+        mask = mask & topo.mask(core, c)
+    ne = bin(mask).count("1")
+
+    def dst(c):
+        a = topo.addr(c)
+        return DstId(rid=a[0], pnc=a[1])
+
+    def to_all(src, name):
+        g.remote_dma_fused([RemoteDMATransfer(dst_ids=[dst(c) for c in peers], dma_engine_mask=mask,
+                                              remote_sem=T.sem[name + "_in"], srcs=[src], dsts=[src for c in peers])],
+                           local_sem=T.sem[name + "_out"])
+        total[name + "_out"] = ne
+        total[name + "_in"] = ne * (N - 1)
+        return (name + "_in", ne * (N - 1))
+
+    lett_ld = done("dl", sy.dma_start(T.wl[:], T.lett[:]), 16)
+    tid_ld = done("dt", s.dma_start(T.tidr[:], T.tid[:]), 16)
+    r_own = done("dr", sy.dma_start(T.rl[me], T.kid[:, 0:32]), 16)
+    kid_ld = []
+    for j in range(8):
+        e = sy if j % 2 == 0 else s
+        kid_ld.append(done("dk%d" % j, e.dma_start(T.kraw[:, 4 * j:4 * j + 4, :], T.kid[j, :]), 16))
+
+    o1 = V(v.memset(T.ones[:], 1.0))
+    V(v.memset(T.wr[:], 0.0))
+    V(v.memset(T.onesf[:], 1.0))
+    V(v.memset(T.zer[:], 0.0))
+    V(v.memset(T.eq[:], 1.0))
+    v0 = V(v.memset(T.acc[:], 0.0))
+    G(g.iota(T.iop[:], [[0, 1]], 0, 1))
+    io = G(g.iota(T.iof[:], [[1, 16]], 0, 0, allow_small_or_imprecise_dtypes=True))
+    wait("g", o1)
+    b1 = G(g.affine_select(T.blk1[:], T.ones[:], [[-16, 8], [0, 16]], A.is_ge, 0.0, 0, 1))
+    wait("g", b1)
+    b2 = G(g.affine_select(T.blk[:], T.blk1[:], [[16, 8], [0, 16]], A.is_ge, 0.0, 15, -1))
+    idn = G(g.affine_select(T.ident[:], T.ones[:], [[-1, 128]], A.is_equal, 0.0, 0, 1))
+
+    wait("v", io)
+    k0 = V(v.tensor_scalar(T.ri[:], T.iop[:], 15, None, A.bitwise_and))
+    wait("v", k0, v0)
+    k1 = V(v.tensor_copy(T.rr[:], T.ri[:]))
+    k2 = V(v.tensor_scalar(T.wsi[:], T.ri[:], 2, None, A.arith_shift_right))
+    wait("v", k2)
+    k3 = V(v.tensor_scalar(T.rm[:], T.iof[:], T.rr[:, 0:1], None, A.is_equal))
+    V(v.tensor_scalar(T.bc[:], T.rr[:], 2.0, 65536.0, A.is_equal, A.mult))
+    k4 = V(v.tensor_copy(T.ws[:], T.wsi[:]))
+    wait("v", k4, b2)
+    for r in range(16):
+        pk = V(v.tensor_scalar(T.pick[:, r, :], T.blk[:], T.rm[:, r:r + 1], None, A.mult))
+    for i in range(4):
+        wrk = V(v.tensor_copy(T.wr[:, i, i::4], T.blk[:, i::4]))
+
+    wait("v", tid_ld)
+    V(v.tensor_scalar(T.ta[:], T.tidr[:], 65280, None, A.bitwise_and))
+    V(v.tensor_scalar(T.tl[:], T.tidr[:], 255, None, A.bitwise_and))
+    a3 = V(v.tensor_scalar(T.tz[:], T.tidr[:], 0, -8388608, A.is_equal, A.mult))
+    wait("v", a3)
+    hi = V(v.tensor_tensor(T.idhi[:], T.ta[:], T.tz[:], A.add))
+    lo = V(v.tensor_copy(T.idlo[:], T.tl[:]))
+    wait("y", hi)
+    hi_st = done("dhi", sy.dma_start(T.idl[me, 0:64, :], T.idhi[:]), 16)
+    wait("s", lo)
+    lo_st = done("dlo", s.dma_start(T.idl[me, 64:128, :], T.idlo[:]), 16)
+
+    wait("g", lett_ld)
+    prev = T.cores[(me - 1) % N]
+    pa = topo.addr(prev)
+    hm = topo.mask(core, prev)
+    hn = bin(hm).count("1")
+    g.remote_dma(out_ap=T.halo[:, 0:8], in_ap=T.wl[:, 0:8], remote_sem=T.sem["halo_in"], local_sem=T.sem["halo_out"],
+                 pid=pa[1], routing_id=pa[0], dma_engine_mask=hm)
+    total["halo_in"] = total["halo_out"] = hn
+    halo_in = ("halo_in", hn)
+    wait("g", r_own)
+    r_in = to_all(T.rl[me], "r")
+
+    wait("v", lett_ld)
+    wb = V(v.tensor_copy(T.wlb[:], T.wl[:]))
+    for j in range(8):
+        wait("v", kid_ld[j])
+        kc = V(v.tensor_scalar(T.kb[:, :, 16 * j:16 * j + 16], T.kraw[:, 4 * j:4 * j + 4, :], 256, None, A.subtract))
+    wait("t", kc, idn)
+    tr = [P(t.matmul(T["p%d" % m][:, 0:128], T.kb[:, m, :], T.ident[:], True, True)) for m in range(4)]
+    ev = [None] * 4
+    for m in (0, 2):
+        wait("s", tr[m])
+        ev[m] = S(s.activation(T.win[:, 512 * me + m:512 * me + 512:4], T["p%d" % m][:, 0:128], F.Copy))
+        wait("v", tr[m + 1])
+        ev[m + 1] = V(v.tensor_copy(T.win[:, 512 * me + m + 1:512 * me + 512:4], T["p%d" % (m + 1)][:, 0:128]))
+    wait("g", hi_st, lo_st)
+    id_in = to_all(T.idl[me], "id")
+    wait("g", ev[2], ev[3])
+    k_in = to_all(T.win[:, 512 * me:512 * me + 512], "k")
+
+    wait("t", pk, wb)
+    for r in range(16):
+        el = P(t.matmul(T.p4[:, r::16], T.pick[:, r, :], T.wlb[:], True, True))
+    for r in range(15):
+        P(t.matmul(T.p5[:, r:80:16], T.pick[:, r + 1, :], T.wlb[:, 0:5], True, True))
+    idz = V(v.memset(T.idwin[:], 0.0))
+    c1 = V(v.tensor_scalar(T.eq[:, 0:4], T.iof[:, 0:4], T.ws[:, 0:1], None, A.is_equal))
+    c2 = V(v.tensor_scalar(T.wq[:], T.wl[:], 1, None, A.arith_shift_right))
+    V(v.tensor_scalar(T.bk[:], T.iof[:, 1:7], T.bc[:, 0:1], None, A.mult))
+    wait("v", c2)
+    c3 = V(v.tensor_tensor(T.dd[:], T.eq[:, 0:4], T.eq[:, 1:5], A.subtract))
+    wait("v", c3)
+    V(v.tensor_scalar(T.d1[:], T.dd[:], 16384.0, None, A.mult))
+    V(v.tensor_scalar(T.d2[:], T.dd[:], 1048576.0, None, A.mult))
+    V(v.tensor_scalar(T.c3[:], T.dd[:, 3:4], 16384.0, 7936.0, A.mult, A.subtract))
+    c4 = V(v.tensor_scalar(T.c4[:], T.dd[:, 3:4], 1048576.0, 2097152.0, A.mult, A.subtract))
+    wait("v", c4)
+    for w in range(3):
+        V(v.tensor_scalar(T.dk[:, w::4], T.zer[:], T.d1[:, w:w + 1], None, A.add))
+        V(v.tensor_scalar(T.dy[:, w::4], T.zer[:], T.d2[:, w:w + 1], None, A.add))
+    V(v.tensor_scalar(T.dk[:, 3::4], T.wq[:], 512.0, T.c3[:, 0:1], A.mult, A.add))
+    dcon = V(v.tensor_scalar(T.dy[:, 3::4], T.zer[:], T.c4[:, 0:1], None, A.add))
+    wait("v", el)
+    em = V(v.tensor_scalar(T.em[:, 0:512], T.p4[:], T.rr[:, 0:1], None, A.is_equal))
+    wait("v", halo_in)
+    hb = V(v.tensor_copy(T.halob[:], T.halo[:]))
+    wait("t", hb)
+    ex = P(t.matmul(T.p5[:, 15:80:16], T.pick[:, 0, :], T.halob[:, 0:5], True, True))
+    wait("v", ex)
+    em = V(v.tensor_scalar(T.em[:, 512:592], T.p5[:, 0:80], T.rr[:, 0:1], None, A.is_equal))
+
+    wait("y", r_in, r_own)
+    rr_ld = done("drr", sy.dma_start(T.rrow[0:8, :], T.rl[:]), 16)
+    wait("v", rr_ld)
+    for j in range(8):
+        rc = V(v.tensor_copy(T.rf[0:8, 16 * j:16 * j + 16], T.rrow[0:8, 32 * j + 16:32 * j + 32]))
+    wait("t", rc)
+    rp = P(t.matmul(T.p6[:, 0:1], T.rf[0:8, :], T.onesf[0:8, :], True, True))
+    wait("v", rp)
+    rcol = V(v.tensor_scalar(T.rcol[:], T.p6[:, 0:1], 256.0, None, A.subtract))
+    wait("v", rcol)
+
+    wait("y", id_in, hi_st, lo_st, idz)
+    wait("s", id_in, hi_st, lo_st, idz)
+    for j in range(N):
+        done("didw", sy.dma_start(T.idwin[0:128:16, 512 * j:512 * j + 512], T.idl[j, 0:64, :]), 16)
+        done("didw", s.dma_start(T.idwin[1:128:16, 512 * j:512 * j + 512], T.idl[j, 64:128, :]), 16)
+    idw = ("didw", total["didw"])
+
+    X = [T.x0, T.x1]
+    SC = [T.sc0, T.sc1]
+    wait("t", *ev)
+
+    def kid_sum(h, tok):
+        wait("t", tok)
+        for i in range(4):
+            r = P(t.matmul(T["p%d" % h][:, 0:64], T.wr[:, i, :], X[h][:, i::4], i == 0, i == 3))
+        return r
+
+    def id_sum(k, h, tok, free):
+        wait("t", tok, free)
+        for i in range(4):
+            r = P(t.matmul(T["p%d" % (2 + k % 2)][:, 64 * h:64 * h + 64], T.wr[:, i, :],
+                           T["y%d" % (2 * (k % 2) + h)][:, i::4], i == 0, i == 3))
+        return r
+
+    xt = [V(v.tensor_scalar(X[h][:], T.em[:, 256 * h:256 * h + 256], T.rcol[:, 0:1], None, A.mult)) for h in range(2)]
+    ks = [kid_sum(h, xt[h]) for h in range(2)]
+    yt, ys, ac = {}, {}, {}
+
+    def accumulate(k):
+        wait("v", ys[k, 1], ac.get(k - 1))
+        ac[k] = V(v.tensor_tensor(T.acc[:], T["p%d" % (2 + k % 2)][:, 0:128], T.acc[:], A.max))
+
+    for k in range(1, 7):
+        lst = T["l%d" % k]
+        for h in range(2):
+            wait("v", ks[h], dcon)
+            a = V(v.tensor_tensor_scan(SC[h][:], T["p%d" % h][:, 0:64], T.dk[:, 64 * h:64 * h + 64], -8192.0, A.max, A.add))
+            wait("v", a)
+            lt = V(v.tensor_scalar(lst[:, 16 * h:16 * h + 16], SC[h][:, 3::4], 8192.0, None, A.add))
+            off = lst[:, 16 * h:16 * h + 16]
+            y = T["y%d" % (2 * (k % 2) + h)]
+            if k < 6:
+                wait("v", lt, k_in, ev[2])
+                xt[h] = V(v.tensor_tensor(X[h][:], T.win[:].indirect(off), T.em[:, 16 * (k + 16 * h):16 * (k + 16 * h) + 256],
+                                          A.mult))
+            if k < 6 or h == 0:
+                wait("s", lt, idw, ys.get((k - 2, h)))
+                yt[k, h] = S(s.activation(y[:], T.idwin[:].indirect(off), F.Identity, bias=T.bk[:, k - 1:k]))
+            else:
+                wait("v", lt, idw, ys.get((k - 2, h)))
+                yt[k, h] = V(v.tensor_scalar(y[:], T.idwin[:].indirect(off), T.bk[:, k - 1:k], None, A.add))
+            if h == 0 and k > 2:
+                accumulate(k - 2)
+            if k < 6:
+                ks[h] = kid_sum(h, xt[h])
+            if k > 1:
+                ys[k - 1, h] = id_sum(k - 1, h, yt[k - 1, h], ac.get(k - 3))
+    for h in range(2):
+        ys[6, h] = id_sum(6, h, yt[6, h], ac[4])
+    accumulate(5)
+    accumulate(6)
+
+    wait("v", ac[6])
+    a = V(v.tensor_tensor_scan(T.scy[:], T.acc[:], T.dy[:], -2097152.0, A.max, A.add))
+    wait("v", a)
+    a = V(v.tensor_scalar(T.keyi[:], T.scy[:, 3::4], 2097152.0, None, A.add))
+    wait("v", a)
+    a = V(v.tensor_scalar(T.leni[:], T.keyi[:], 16, None, A.arith_shift_right))
+    b = V(v.tensor_scalar(T.idi[:], T.keyi[:], 65535, None, A.bitwise_and))
+    wait("v", a)
+    a = V(v.tensor_copy(T.yl[:], T.leni[:]))
+    wait("v", b)
+    b = V(v.tensor_copy(T.yi[:], T.idi[:]))
+    wait("y", a)
+    done("dyl", sy.dma_start(T.ylen[:], T.yl[:]), 16)
+    wait("s", b)
+    done("dyi", s.dma_start(T.yid[:], T.yi[:]), 16)
+    for name in SEMAPHORES:
+        wait("g", (name, total[name]))

@@ -4,7 +4,7 @@ from concourse.mybir import AluOpType as A, ActivationFunctionType as F
 N = 8
 SCRATCH = {
     "kraw": ("sbuf", [128, 32, 16], "int32"),
-    "kb": ("sbuf", [128, 4, 128], "bfloat16"),
+    "kb": ("sbuf", [128, 8, 64], "bfloat16"),
     "win": ("sbuf", [128, 4096], "bfloat16"),
     "idwin": ("sbuf", [128, 4096], "bfloat16"),
     "wl": ("sbuf", [128, 32], "int32"),
@@ -25,7 +25,6 @@ SCRATCH = {
     "ones": ("sbuf", [128, 128], "bfloat16"),
     "blk1": ("sbuf", [128, 128], "bfloat16"),
     "blk": ("sbuf", [128, 128], "bfloat16"),
-    "ident": ("sbuf", [128, 128], "bfloat16"),
     "wr": ("sbuf", [128, 4, 128], "bfloat16"),
     "pick": ("sbuf", [128, 16, 128], "bfloat16"),
     "iop": ("sbuf", [128, 1], "int32"),
@@ -68,7 +67,7 @@ for _k in range(4):
 for _k in range(7):
     SCRATCH["p%d" % _k] = ("psum", [128, 512], "float32")
 SEMAPHORES = ["cv", "cs", "ct", "cg", "dl", "dr", "dt", "dhi", "dlo", "drr", "didw", "dyl", "dyi",
-              "halo_in", "r_in", "id_in", "k_in", "halo_out", "r_out", "id_out", "k_out"] + ["dk%d" % k for k in range(8)]
+              "halo_in", "r_in", "id_in", "k_in", "halo_out", "r_out", "id_out", "k_out"] + ["dk%d" % k for k in range(4)]
 
 
 def rank_program(g, core, T, topo):
@@ -116,38 +115,46 @@ def rank_program(g, core, T, topo):
     tid_ld = done("dt", s.dma_start(T.tidr[:], T.tid[:]), 16)
     r_own = done("dr", sy.dma_start(T.rl[me], T.kid[:, 0:32]), 16)
     kid_ld = []
-    for j in range(8):
-        e = sy if j % 2 == 0 else s
-        kid_ld.append(done("dk%d" % j, e.dma_start(T.kraw[:, 4 * j:4 * j + 4, :], T.kid[j, :]), 16))
+    for j in range(4):
+        a, gl = j // 2, j % 2
+        kid_ld.append(done("dk%d" % j, (sy, s)[gl].dma_start(T.kraw[:, 16 * gl + 8 * a:16 * gl + 8 * a + 8, :],
+                                                             T.kid[gl::2, 4096 * a:4096 * a + 4096]), 16))
 
     o1 = V(v.memset(T.ones[:], 1.0))
     V(v.memset(T.wr[:], 0.0))
     V(v.memset(T.onesf[:], 1.0))
     V(v.memset(T.zer[:], 0.0))
     V(v.memset(T.eq[:], 1.0))
-    v0 = V(v.memset(T.acc[:], 0.0))
+    V(v.memset(T.acc[:], 0.0))
+    idz = V(v.memset(T.idwin[:, 0:1024], 0.0))
+    wait("s", idz)
+    for j in range(1, 4):
+        idz = S(s.activation(T.idwin[:, 1024 * j:1024 * j + 1024], T.idwin[:, 0:1024], F.Copy))
     G(g.iota(T.iop[:], [[0, 1]], 0, 1))
     io = G(g.iota(T.iof[:], [[1, 16]], 0, 0, allow_small_or_imprecise_dtypes=True))
     wait("g", o1)
     b1 = G(g.affine_select(T.blk1[:], T.ones[:], [[-16, 8], [0, 16]], A.is_ge, 0.0, 0, 1))
     wait("g", b1)
     b2 = G(g.affine_select(T.blk[:], T.blk1[:], [[16, 8], [0, 16]], A.is_ge, 0.0, 15, -1))
-    idn = G(g.affine_select(T.ident[:], T.ones[:], [[-1, 128]], A.is_equal, 0.0, 0, 1))
 
     wait("v", io)
     k0 = V(v.tensor_scalar(T.ri[:], T.iop[:], 15, None, A.bitwise_and))
-    wait("v", k0, v0)
-    k1 = V(v.tensor_copy(T.rr[:], T.ri[:]))
+    wait("v", k0)
+    V(v.tensor_copy(T.rr[:], T.ri[:]))
     k2 = V(v.tensor_scalar(T.wsi[:], T.ri[:], 2, None, A.arith_shift_right))
     wait("v", k2)
-    k3 = V(v.tensor_scalar(T.rm[:], T.iof[:], T.rr[:, 0:1], None, A.is_equal))
+    V(v.tensor_scalar(T.rm[:], T.iof[:], T.rr[:, 0:1], None, A.is_equal))
     V(v.tensor_scalar(T.bc[:], T.rr[:], 2.0, 65536.0, A.is_equal, A.mult))
     k4 = V(v.tensor_copy(T.ws[:], T.wsi[:]))
     wait("v", k4, b2)
-    for r in range(16):
-        pk = V(v.tensor_scalar(T.pick[:, r, :], T.blk[:], T.rm[:, r:r + 1], None, A.mult))
+
+    def picks(lo, hi):
+        for r in range(lo, hi):
+            pk = V(v.tensor_scalar(T.pick[:, r, :], T.blk[:], T.rm[:, r:r + 1], None, A.mult))
+        return pk
+    picks(0, 8)
     for i in range(4):
-        wrk = V(v.tensor_copy(T.wr[:, i, i::4], T.blk[:, i::4]))
+        V(v.tensor_copy(T.wr[:, i, i::4], T.blk[:, i::4]))
 
     wait("v", tid_ld)
     V(v.tensor_scalar(T.ta[:], T.tidr[:], 65280, None, A.bitwise_and))
@@ -158,8 +165,8 @@ def rank_program(g, core, T, topo):
     lo = V(v.tensor_copy(T.idlo[:], T.tl[:]))
     wait("y", hi)
     hi_st = done("dhi", sy.dma_start(T.idl[me, 0:64, :], T.idhi[:]), 16)
-    wait("s", lo)
-    lo_st = done("dlo", s.dma_start(T.idl[me, 64:128, :], T.idlo[:]), 16)
+    wait("y", lo)
+    lo_st = done("dlo", sy.dma_start(T.idl[me, 64:128, :], T.idlo[:]), 16)
 
     wait("g", lett_ld)
     prev = T.cores[(me - 1) % N]
@@ -175,20 +182,18 @@ def rank_program(g, core, T, topo):
 
     wait("v", lett_ld)
     wb = V(v.tensor_copy(T.wlb[:], T.wl[:]))
-    for j in range(8):
+    pk = picks(8, 16)
+    for j in range(4):
+        a, gl = j // 2, j % 2
         wait("v", kid_ld[j])
-        kc = V(v.tensor_scalar(T.kb[:, :, 16 * j:16 * j + 16], T.kraw[:, 4 * j:4 * j + 4, :], 256, None, A.subtract))
-    wait("t", kc, idn)
-    tr = [P(t.matmul(T["p%d" % m][:, 0:128], T.kb[:, m, :], T.ident[:], True, True)) for m in range(4)]
-    ev = [None] * 4
-    for m in (0, 2):
-        wait("s", tr[m])
-        ev[m] = S(s.activation(T.win[:, 512 * me + m:512 * me + 512:4], T["p%d" % m][:, 0:128], F.Copy))
-        wait("v", tr[m + 1])
-        ev[m + 1] = V(v.tensor_copy(T.win[:, 512 * me + m + 1:512 * me + 512:4], T["p%d" % (m + 1)][:, 0:128]))
+        kc = V(v.tensor_scalar(T.kb[:, :, 32 * a + 16 * gl:32 * a + 16 * gl + 16],
+                               T.kraw[:, 16 * gl + 8 * a:16 * gl + 8 * a + 8, :], 256, None, A.subtract))
+    wait("v", kc)
+    for m in range(8):
+        ev = V(v.transpose(T.win[:, 512 * me + m:512 * me + 512:8], T.kb[:, m, :]))
     wait("g", hi_st, lo_st)
     id_in = to_all(T.idl[me], "id")
-    wait("g", ev[2], ev[3])
+    wait("g", ev)
     k_in = to_all(T.win[:, 512 * me:512 * me + 512], "k")
 
     wait("t", pk, wb)
@@ -196,8 +201,7 @@ def rank_program(g, core, T, topo):
         el = P(t.matmul(T.p4[:, r::16], T.pick[:, r, :], T.wlb[:], True, True))
     for r in range(15):
         P(t.matmul(T.p5[:, r:80:16], T.pick[:, r + 1, :], T.wlb[:, 0:5], True, True))
-    idz = V(v.memset(T.idwin[:], 0.0))
-    c1 = V(v.tensor_scalar(T.eq[:, 0:4], T.iof[:, 0:4], T.ws[:, 0:1], None, A.is_equal))
+    V(v.tensor_scalar(T.eq[:, 0:4], T.iof[:, 0:4], T.ws[:, 0:1], None, A.is_equal))
     c2 = V(v.tensor_scalar(T.wq[:], T.wl[:], 1, None, A.arith_shift_right))
     V(v.tensor_scalar(T.bk[:], T.iof[:, 1:7], T.bc[:, 0:1], None, A.mult))
     wait("v", c2)
@@ -214,13 +218,13 @@ def rank_program(g, core, T, topo):
     V(v.tensor_scalar(T.dk[:, 3::4], T.wq[:], 512.0, T.c3[:, 0:1], A.mult, A.add))
     dcon = V(v.tensor_scalar(T.dy[:, 3::4], T.zer[:], T.c4[:, 0:1], None, A.add))
     wait("v", el)
-    em = V(v.tensor_scalar(T.em[:, 0:512], T.p4[:], T.rr[:, 0:1], None, A.is_equal))
+    V(v.tensor_scalar(T.em[:, 0:512], T.p4[:], T.rr[:, 0:1], None, A.is_equal))
     wait("v", halo_in)
     hb = V(v.tensor_copy(T.halob[:], T.halo[:]))
     wait("t", hb)
     ex = P(t.matmul(T.p5[:, 15:80:16], T.pick[:, 0, :], T.halob[:, 0:5], True, True))
     wait("v", ex)
-    em = V(v.tensor_scalar(T.em[:, 512:592], T.p5[:, 0:80], T.rr[:, 0:1], None, A.is_equal))
+    V(v.tensor_scalar(T.em[:, 512:592], T.p5[:, 0:80], T.rr[:, 0:1], None, A.is_equal))
 
     wait("y", r_in, r_own)
     rr_ld = done("drr", sy.dma_start(T.rrow[0:8, :], T.rl[:]), 16)
@@ -242,7 +246,6 @@ def rank_program(g, core, T, topo):
 
     X = [T.x0, T.x1]
     SC = [T.sc0, T.sc1]
-    wait("t", *ev)
 
     def kid_sum(h, tok):
         wait("t", tok)
@@ -275,7 +278,7 @@ def rank_program(g, core, T, topo):
             off = lst[:, 16 * h:16 * h + 16]
             y = T["y%d" % (2 * (k % 2) + h)]
             if k < 6:
-                wait("v", lt, k_in, ev[2])
+                wait("v", lt, k_in, ev)
                 xt[h] = V(v.tensor_tensor(X[h][:], T.win[:].indirect(off), T.em[:, 16 * (k + 16 * h):16 * (k + 16 * h) + 256],
                                           A.mult))
             if k < 6 or h == 0:

@@ -9,16 +9,16 @@ SCRATCH = {
     "idwin": ("sbuf", [128, 4096], "bfloat16"),
     "wl": ("sbuf", [128, 32], "int32"),
     "wlb": ("sbuf", [128, 32], "bfloat16"),
-    "halo": ("sbuf", [128, 8], "int32"),
+    "halo": ("sbuf", [128, 16], "int32"),
     "halob": ("sbuf", [128, 8], "bfloat16"),
     "wq": ("sbuf", [128, 32], "int32"),
-    "tidr": ("sbuf", [128, 32], "int32"),
-    "ta": ("sbuf", [128, 32], "int32"),
-    "tz": ("sbuf", [128, 32], "int32"),
-    "tl": ("sbuf", [128, 32], "int32"),
-    "idhi": ("sbuf", [128, 32], "bfloat16"),
-    "idlo": ("sbuf", [128, 32], "bfloat16"),
-    "rrow": ("sbuf", [128, 256], "int32"),
+    "tidr": ("sbuf", [128, 64], "int32"),
+    "ta": ("sbuf", [128, 64], "int32"),
+    "tz": ("sbuf", [128, 64], "int32"),
+    "tl": ("sbuf", [128, 64], "int32"),
+    "idhi": ("sbuf", [128, 64], "bfloat16"),
+    "idlo": ("sbuf", [128, 64], "bfloat16"),
+    "rrow": ("sbuf", [128, 128], "int32"),
     "rf": ("sbuf", [128, 128], "float32"),
     "onesf": ("sbuf", [128, 1], "float32"),
     "rcol": ("sbuf", [128, 1], "float32"),
@@ -26,6 +26,7 @@ SCRATCH = {
     "blk1": ("sbuf", [128, 128], "bfloat16"),
     "blk": ("sbuf", [128, 128], "bfloat16"),
     "wr": ("sbuf", [128, 4, 128], "bfloat16"),
+    "wi": ("sbuf", [128, 8, 128], "bfloat16"),
     "pick": ("sbuf", [128, 16, 128], "bfloat16"),
     "iop": ("sbuf", [128, 1], "int32"),
     "iof": ("sbuf", [128, 16], "float32"),
@@ -40,18 +41,23 @@ SCRATCH = {
     "d2": ("sbuf", [128, 4], "float32"),
     "c3": ("sbuf", [128, 1], "float32"),
     "c4": ("sbuf", [128, 1], "float32"),
+    "lowr": ("sbuf", [128, 1], "float32"),
+    "e0": ("sbuf", [128, 1], "float32"),
+    "e1": ("sbuf", [128, 1], "float32"),
     "bc": ("sbuf", [128, 1], "float32"),
     "bk": ("sbuf", [128, 6], "float32"),
     "zer": ("sbuf", [128, 32], "float32"),
     "dk": ("sbuf", [128, 128], "float32"),
-    "dy": ("sbuf", [128, 128], "float32"),
+    "dz": ("sbuf", [128, 64], "float32"),
+    "dy": ("sbuf", [128, 320], "float32"),
     "em": ("sbuf", [128, 592], "bfloat16"),
     "x0": ("sbuf", [128, 256], "bfloat16"),
     "x1": ("sbuf", [128, 256], "bfloat16"),
     "sc0": ("sbuf", [128, 64], "float32"),
     "sc1": ("sbuf", [128, 64], "float32"),
-    "scy": ("sbuf", [128, 128], "float32"),
-    "acc": ("sbuf", [128, 128], "float32"),
+    "scy": ("sbuf", [128, 320], "float32"),
+    "scz": ("sbuf", [128, 128], "float32"),
+    "best": ("sbuf", [128, 32], "float32"),
     "keyi": ("sbuf", [128, 32], "int32"),
     "leni": ("sbuf", [128, 32], "int32"),
     "idi": ("sbuf", [128, 32], "int32"),
@@ -62,12 +68,11 @@ SCRATCH = {
 }
 for _k in range(1, 7):
     SCRATCH["l%d" % _k] = ("sbuf", [128, 32], "uint16")
-for _k in range(4):
-    SCRATCH["y%d" % _k] = ("sbuf", [128, 256], "bfloat16")
-for _k in range(7):
+    SCRATCH["y%d" % _k] = ("sbuf", [128, 512], "bfloat16")
+for _k in range(8):
     SCRATCH["p%d" % _k] = ("psum", [128, 512], "float32")
 SEMAPHORES = ["cv", "cs", "ct", "cg", "dl", "dr", "dt", "dhi", "dlo", "drr", "didw", "dyl", "dyi",
-              "halo_in", "r_in", "id_in", "k_in", "halo_out", "r_out", "id_out", "k_out"] + ["dk%d" % k for k in range(4)]
+              "r_in", "id_in", "k_in", "r_out", "id_out", "k_out"] + ["dk%d" % k for k in range(4)]
 
 
 def rank_program(g, core, T, topo):
@@ -111,25 +116,27 @@ def rank_program(g, core, T, topo):
         total[name + "_in"] = ne * (N - 1)
         return (name + "_in", ne * (N - 1))
 
-    lett_ld = done("dl", sy.dma_start(T.wl[:], T.lett[:]), 16)
-    tid_ld = done("dt", s.dma_start(T.tidr[:], T.tid[:]), 16)
-    r_own = done("dr", sy.dma_start(T.rl[me], T.kid[:, 0:32]), 16)
+    done("dr", sy.dma_start(T.rl[me, 0:64, :], T.kid[:, 16:32]), 16)
+    r_own = done("dr", sy.dma_start(T.rl[me, 64:128, :], T.lett[:, 0:16]), 16)
+    tid_ld = done("dt", s.dma_start(T.tidr[0:64, :], T.tid[:]), 16)
     kid_ld = []
     for j in range(4):
         a, gl = j // 2, j % 2
-        kid_ld.append(done("dk%d" % j, (sy, s)[gl].dma_start(T.kraw[:, 16 * gl + 8 * a:16 * gl + 8 * a + 8, :],
+        kid_ld.append(done("dk%d" % j, (s, sy)[gl].dma_start(T.kraw[:, 16 * gl + 8 * a:16 * gl + 8 * a + 8, :],
                                                              T.kid[gl::2, 4096 * a:4096 * a + 4096]), 16))
+    lett_ld = done("dl", sy.dma_start(T.wl[:], T.lett[:]), 16)
 
     o1 = V(v.memset(T.ones[:], 1.0))
+    idz = V(v.memset(T.idwin[:, 0:512], 0.0))
+    wait("s", idz)
+    for n in (512, 1024, 2048):
+        idz = S(s.activation(T.idwin[:, n:2 * n], T.idwin[:, 0:n], F.Copy))
+        wait("s", idz)
     V(v.memset(T.wr[:], 0.0))
     V(v.memset(T.onesf[:], 1.0))
     V(v.memset(T.zer[:], 0.0))
     V(v.memset(T.eq[:], 1.0))
-    V(v.memset(T.acc[:], 0.0))
-    idz = V(v.memset(T.idwin[:, 0:1024], 0.0))
-    wait("s", idz)
-    for j in range(1, 4):
-        idz = S(s.activation(T.idwin[:, 1024 * j:1024 * j + 1024], T.idwin[:, 0:1024], F.Copy))
+    hz = V(v.memset(T.halo[:], 0))
     G(g.iota(T.iop[:], [[0, 1]], 0, 1))
     io = G(g.iota(T.iof[:], [[1, 16]], 0, 0, allow_small_or_imprecise_dtypes=True))
     wait("g", o1)
@@ -146,43 +153,32 @@ def rank_program(g, core, T, topo):
     V(v.tensor_scalar(T.rm[:], T.iof[:], T.rr[:, 0:1], None, A.is_equal))
     V(v.tensor_scalar(T.bc[:], T.rr[:], 2.0, 65536.0, A.is_equal, A.mult))
     k4 = V(v.tensor_copy(T.ws[:], T.wsi[:]))
+
+    wait("v", tid_ld)
+    V(v.tensor_scalar(T.ta[0:64, :], T.tidr[0:64, :], 65280, None, A.bitwise_and))
+    a3 = V(v.tensor_scalar(T.tz[0:64, :], T.tidr[0:64, :], 0, -524288, A.is_equal, A.mult))
+    a4 = V(v.tensor_scalar(T.tl[0:64, :], T.tidr[0:64, :], 255, None, A.bitwise_and))
+    wait("v", a3)
+    hi = V(v.tensor_tensor(T.idhi[0:64, :], T.ta[0:64, :], T.tz[0:64, :], A.add))
+    wait("v", a4)
+    lo = V(v.tensor_copy(T.idlo[0:64, :], T.tl[0:64, :]))
+    wait("y", hi)
+    hi_st = done("dhi", sy.dma_start(T.idl[me, 0:64, :], T.idhi[0:64, :]), 16)
+    wait("y", lo)
+    lo_st = done("dlo", sy.dma_start(T.idl[me, 64:128, :], T.idlo[0:64, :]), 16)
+
+    wait("g", r_own)
+    r_in = to_all(T.rl[me], "r")
+
     wait("v", k4, b2)
 
     def picks(lo, hi):
         for r in range(lo, hi):
             pk = V(v.tensor_scalar(T.pick[:, r, :], T.blk[:], T.rm[:, r:r + 1], None, A.mult))
         return pk
-    picks(0, 8)
     for i in range(4):
         V(v.tensor_copy(T.wr[:, i, i::4], T.blk[:, i::4]))
-
-    wait("v", tid_ld)
-    V(v.tensor_scalar(T.ta[:], T.tidr[:], 65280, None, A.bitwise_and))
-    V(v.tensor_scalar(T.tl[:], T.tidr[:], 255, None, A.bitwise_and))
-    a3 = V(v.tensor_scalar(T.tz[:], T.tidr[:], 0, -8388608, A.is_equal, A.mult))
-    wait("v", a3)
-    hi = V(v.tensor_tensor(T.idhi[:], T.ta[:], T.tz[:], A.add))
-    lo = V(v.tensor_copy(T.idlo[:], T.tl[:]))
-    wait("y", hi)
-    hi_st = done("dhi", sy.dma_start(T.idl[me, 0:64, :], T.idhi[:]), 16)
-    wait("y", lo)
-    lo_st = done("dlo", sy.dma_start(T.idl[me, 64:128, :], T.idlo[:]), 16)
-
-    wait("g", lett_ld)
-    prev = T.cores[(me - 1) % N]
-    pa = topo.addr(prev)
-    hm = topo.mask(core, prev)
-    hn = bin(hm).count("1")
-    g.remote_dma(out_ap=T.halo[:, 0:8], in_ap=T.wl[:, 0:8], remote_sem=T.sem["halo_in"], local_sem=T.sem["halo_out"],
-                 pid=pa[1], routing_id=pa[0], dma_engine_mask=hm)
-    total["halo_in"] = total["halo_out"] = hn
-    halo_in = ("halo_in", hn)
-    wait("g", r_own)
-    r_in = to_all(T.rl[me], "r")
-
-    wait("v", lett_ld)
-    wb = V(v.tensor_copy(T.wlb[:], T.wl[:]))
-    pk = picks(8, 16)
+    picks(0, 8)
     for j in range(4):
         a, gl = j // 2, j % 2
         wait("v", kid_ld[j])
@@ -196,6 +192,9 @@ def rank_program(g, core, T, topo):
     wait("g", ev)
     k_in = to_all(T.win[:, 512 * me:512 * me + 512], "k")
 
+    pk = picks(8, 16)
+    wait("v", lett_ld)
+    wb = V(v.tensor_copy(T.wlb[:], T.wl[:]))
     wait("t", pk, wb)
     for r in range(16):
         el = P(t.matmul(T.p4[:, r::16], T.pick[:, r, :], T.wlb[:], True, True))
@@ -204,37 +203,47 @@ def rank_program(g, core, T, topo):
     V(v.tensor_scalar(T.eq[:, 0:4], T.iof[:, 0:4], T.ws[:, 0:1], None, A.is_equal))
     c2 = V(v.tensor_scalar(T.wq[:], T.wl[:], 1, None, A.arith_shift_right))
     V(v.tensor_scalar(T.bk[:], T.iof[:, 1:7], T.bc[:, 0:1], None, A.mult))
+    c1 = V(v.tensor_scalar(T.lowr[:], T.ws[:], 2.0, None, A.is_lt))
+    V(v.memset(T.dy[:], 0.0))
     wait("v", c2)
     c3 = V(v.tensor_tensor(T.dd[:], T.eq[:, 0:4], T.eq[:, 1:5], A.subtract))
+    wait("v", c1)
+    V(v.tensor_scalar(T.e0[:], T.lowr[:], 2097152.0, 1048576.0, A.mult, A.subtract))
+    V(v.tensor_scalar(T.e1[:], T.lowr[:], -1048576.0, 2097152.0, A.mult, A.subtract))
     wait("v", c3)
     V(v.tensor_scalar(T.d1[:], T.dd[:], 16384.0, None, A.mult))
     V(v.tensor_scalar(T.d2[:], T.dd[:], 1048576.0, None, A.mult))
     V(v.tensor_scalar(T.c3[:], T.dd[:, 3:4], 16384.0, 7936.0, A.mult, A.subtract))
     c4 = V(v.tensor_scalar(T.c4[:], T.dd[:, 3:4], 1048576.0, 2097152.0, A.mult, A.subtract))
     wait("v", c4)
-    for w in range(3):
-        V(v.tensor_scalar(T.dk[:, w::4], T.zer[:], T.d1[:, w:w + 1], None, A.add))
-        V(v.tensor_scalar(T.dy[:, w::4], T.zer[:], T.d2[:, w:w + 1], None, A.add))
-    V(v.tensor_scalar(T.dk[:, 3::4], T.wq[:], 512.0, T.c3[:, 0:1], A.mult, A.add))
-    dcon = V(v.tensor_scalar(T.dy[:, 3::4], T.zer[:], T.c4[:, 0:1], None, A.add))
+    for w in range(4):
+        if w < 3:
+            V(v.tensor_scalar(T.dk[:, w::4], T.zer[:], T.d1[:, w:w + 1], None, A.add))
+        V(v.tensor_scalar(T.dz[:, w::4], T.zer[:, 0:16], T.d2[:, w:w + 1] if w < 3 else T.c4[:, 0:1], None, A.add))
+    V(v.tensor_scalar(T.dy[:, 4::10], T.zer[:], T.e0[:, 0:1], None, A.add))
+    V(v.tensor_scalar(T.dy[:, 9::10], T.zer[:], T.e1[:, 0:1], None, A.add))
+    dcon = V(v.tensor_scalar(T.dk[:, 3::4], T.wq[:], 512.0, T.c3[:, 0:1], A.mult, A.add))
     wait("v", el)
     V(v.tensor_scalar(T.em[:, 0:512], T.p4[:], T.rr[:, 0:1], None, A.is_equal))
-    wait("v", halo_in)
-    hb = V(v.tensor_copy(T.halob[:], T.halo[:]))
-    wait("t", hb)
-    ex = P(t.matmul(T.p5[:, 15:80:16], T.pick[:, 0, :], T.halob[:, 0:5], True, True))
-    wait("v", ex)
-    V(v.tensor_scalar(T.em[:, 512:592], T.p5[:, 0:80], T.rr[:, 0:1], None, A.is_equal))
+    wz = V(v.memset(T.wi[:], 0.0))
+    wait("v", wz)
+    for i in range(8):
+        wi = V(v.tensor_copy(T.wi[:, i, i::8], T.blk[:, i::8]))
 
-    wait("y", r_in, r_own)
-    rr_ld = done("drr", sy.dma_start(T.rrow[0:8, :], T.rl[:]), 16)
+    wait("y", r_in, r_own, hz)
+    done("drr", sy.dma_start(T.rrow[0:8, :], T.rl[:, 0:64, :]), 16)
+    rr_ld = done("drr", sy.dma_start(T.halo[0:128:16, :], T.rl[(me + 1) % N, 64:128, :]), 16)
     wait("v", rr_ld)
-    for j in range(8):
-        rc = V(v.tensor_copy(T.rf[0:8, 16 * j:16 * j + 16], T.rrow[0:8, 32 * j + 16:32 * j + 32]))
+    rc = V(v.tensor_copy(T.rf[0:8, :], T.rrow[0:8, :]))
+    hb = V(v.tensor_copy(T.halob[:], T.halo[:, 0:8]))
     wait("t", rc)
     rp = P(t.matmul(T.p6[:, 0:1], T.rf[0:8, :], T.onesf[0:8, :], True, True))
+    wait("t", hb)
+    ex = P(t.matmul(T.p5[:, 15:80:16], T.pick[:, 0, :], T.halob[:, 0:5], True, True))
     wait("v", rp)
     rcol = V(v.tensor_scalar(T.rcol[:], T.p6[:, 0:1], 256.0, None, A.subtract))
+    wait("v", ex)
+    V(v.tensor_scalar(T.em[:, 512:592], T.p5[:, 0:80], T.rr[:, 0:1], None, A.is_equal))
     wait("v", rcol)
 
     wait("y", id_in, hi_st, lo_st, idz)
@@ -253,20 +262,16 @@ def rank_program(g, core, T, topo):
             r = P(t.matmul(T["p%d" % h][:, 0:64], T.wr[:, i, :], X[h][:, i::4], i == 0, i == 3))
         return r
 
-    def id_sum(k, h, tok, free):
-        wait("t", tok, free)
-        for i in range(4):
-            r = P(t.matmul(T["p%d" % (2 + k % 2)][:, 64 * h:64 * h + 64], T.wr[:, i, :],
-                           T["y%d" % (2 * (k % 2) + h)][:, i::4], i == 0, i == 3))
-        return r
-
     xt = [V(v.tensor_scalar(X[h][:], T.em[:, 256 * h:256 * h + 256], T.rcol[:, 0:1], None, A.mult)) for h in range(2)]
     ks = [kid_sum(h, xt[h]) for h in range(2)]
-    yt, ys, ac = {}, {}, {}
+    yt, ys = {}, {}
 
-    def accumulate(k):
-        wait("v", ys[k, 1], ac.get(k - 1))
-        ac[k] = V(v.tensor_tensor(T.acc[:], T["p%d" % (2 + k % 2)][:, 0:128], T.acc[:], A.max))
+    def id_sum(k, part):
+        if k < 1:
+            return
+        wait("t", yt[k, 0], yt[k, 1], wi)
+        for i in range(4 * part, 4 * part + 4):
+            ys[k] = P(t.matmul(T.p2[:, k - 1:320:5], T.wi[:, i, :], T["y%d" % k][:, i::8], i == 0, i == 7))
 
     for k in range(1, 7):
         lst = T["l%d" % k]
@@ -276,37 +281,41 @@ def rank_program(g, core, T, topo):
             wait("v", a)
             lt = V(v.tensor_scalar(lst[:, 16 * h:16 * h + 16], SC[h][:, 3::4], 8192.0, None, A.add))
             off = lst[:, 16 * h:16 * h + 16]
-            y = T["y%d" % (2 * (k % 2) + h)]
+            y, bias = T["y%d" % k][:, 256 * h:256 * h + 256], T.bk[:, k - 1:k]
             if k < 6:
                 wait("v", lt, k_in, ev)
                 xt[h] = V(v.tensor_tensor(X[h][:], T.win[:].indirect(off), T.em[:, 16 * (k + 16 * h):16 * (k + 16 * h) + 256],
                                           A.mult))
-            if k < 6 or h == 0:
-                wait("s", lt, idw, ys.get((k - 2, h)))
-                yt[k, h] = S(s.activation(y[:], T.idwin[:].indirect(off), F.Identity, bias=T.bk[:, k - 1:k]))
-            else:
-                wait("v", lt, idw, ys.get((k - 2, h)))
-                yt[k, h] = V(v.tensor_scalar(y[:], T.idwin[:].indirect(off), T.bk[:, k - 1:k], None, A.add))
-            if h == 0 and k > 2:
-                accumulate(k - 2)
-            if k < 6:
                 ks[h] = kid_sum(h, xt[h])
-            if k > 1:
-                ys[k - 1, h] = id_sum(k - 1, h, yt[k - 1, h], ac.get(k - 3))
+            if k < 6 or h == 0:
+                wait("s", lt, idw)
+                yt[k, h] = S(s.activation(y, T.idwin[:].indirect(off), F.Identity, bias=bias))
+            else:
+                wait("v", lt, idw)
+                yt[k, h] = V(v.tensor_scalar(y, T.idwin[:].indirect(off), bias, None, A.add))
+            id_sum(k - 2, h)
+    for part in range(2):
+        id_sum(5, part)
     for h in range(2):
-        ys[6, h] = id_sum(6, h, yt[6, h], ac[4])
-    accumulate(5)
-    accumulate(6)
+        wait("t", yt[6, h])
+        for i in range(4):
+            ys[6, h] = P(t.matmul(T["p%d" % (4 + h)][:, 0:64], T.wr[:, i, :], T.y6[:, 256 * h + i:256 * h + 256:4], i == 0, i == 3))
 
-    wait("v", ac[6])
-    a = V(v.tensor_tensor_scan(T.scy[:], T.acc[:], T.dy[:], -2097152.0, A.max, A.add))
+    wait("v", ys[5])
+    a = V(v.tensor_tensor_scan(T.scy[:], T.p2[:, 0:320], T.dy[:], -2097152.0, A.max, A.add))
     wait("v", a)
-    a = V(v.tensor_scalar(T.keyi[:], T.scy[:, 3::4], 2097152.0, None, A.add))
+    V(v.tensor_scalar(T.best[:], T.scy[:, 9::10], -2097152.0, None, A.max))
+    for h in range(2):
+        c = slice(64 * h, 64 * h + 64)
+        wait("v", ys[6, h])
+        a = V(v.tensor_tensor_scan(T.scz[:, c], T["p%d" % (4 + h)][:, 0:64], T.dz[:], -2097152.0, A.max, A.add))
+    wait("v", a)
+    a = V(v.tensor_tensor(T.keyi[:], T.best[:], T.scz[:, 3::4], A.max))
     wait("v", a)
     a = V(v.tensor_scalar(T.leni[:], T.keyi[:], 16, None, A.arith_shift_right))
     b = V(v.tensor_scalar(T.idi[:], T.keyi[:], 65535, None, A.bitwise_and))
     wait("v", a)
-    a = V(v.tensor_copy(T.yl[:], T.leni[:]))
+    a = V(v.tensor_scalar(T.yl[:], T.leni[:], 32, None, A.add))
     wait("v", b)
     b = V(v.tensor_copy(T.yi[:], T.idi[:]))
     wait("y", a)

@@ -2,77 +2,24 @@ from concourse.bass import DstId, RemoteDMATransfer
 from concourse.mybir import AluOpType as A, ActivationFunctionType as F
 
 N = 8
-SCRATCH = {
-    "kraw": ("sbuf", [128, 32, 16], "int32"),
-    "kb": ("sbuf", [128, 8, 64], "bfloat16"),
-    "win": ("sbuf", [128, 4096], "bfloat16"),
-    "idwin": ("sbuf", [128, 4096], "bfloat16"),
-    "wl": ("sbuf", [128, 32], "int32"),
-    "wlb": ("sbuf", [128, 32], "bfloat16"),
-    "halo": ("sbuf", [128, 16], "int32"),
-    "halob": ("sbuf", [128, 8], "bfloat16"),
-    "wq": ("sbuf", [128, 32], "int32"),
-    "tidr": ("sbuf", [128, 64], "int32"),
-    "ta": ("sbuf", [128, 64], "int32"),
-    "tz": ("sbuf", [128, 64], "int32"),
-    "tl": ("sbuf", [128, 64], "int32"),
-    "idhi": ("sbuf", [128, 64], "bfloat16"),
-    "idlo": ("sbuf", [128, 64], "bfloat16"),
-    "rrow": ("sbuf", [128, 128], "int32"),
-    "rf": ("sbuf", [128, 128], "float32"),
-    "onesf": ("sbuf", [128, 1], "float32"),
-    "rcol": ("sbuf", [128, 1], "float32"),
-    "ones": ("sbuf", [128, 128], "bfloat16"),
-    "blk1": ("sbuf", [128, 128], "bfloat16"),
-    "blk": ("sbuf", [128, 128], "bfloat16"),
-    "wr": ("sbuf", [128, 4, 128], "bfloat16"),
-    "wi": ("sbuf", [128, 8, 128], "bfloat16"),
-    "pick": ("sbuf", [128, 16, 128], "bfloat16"),
-    "iop": ("sbuf", [128, 1], "int32"),
-    "iof": ("sbuf", [128, 16], "float32"),
-    "ri": ("sbuf", [128, 1], "int32"),
-    "rr": ("sbuf", [128, 1], "float32"),
-    "wsi": ("sbuf", [128, 1], "int32"),
-    "ws": ("sbuf", [128, 1], "float32"),
-    "rm": ("sbuf", [128, 16], "float32"),
-    "eq": ("sbuf", [128, 8], "float32"),
-    "dd": ("sbuf", [128, 4], "float32"),
-    "d1": ("sbuf", [128, 4], "float32"),
-    "d2": ("sbuf", [128, 4], "float32"),
-    "c3": ("sbuf", [128, 1], "float32"),
-    "c4": ("sbuf", [128, 1], "float32"),
-    "lowr": ("sbuf", [128, 1], "float32"),
-    "e0": ("sbuf", [128, 1], "float32"),
-    "e1": ("sbuf", [128, 1], "float32"),
-    "bc": ("sbuf", [128, 1], "float32"),
-    "bk": ("sbuf", [128, 6], "float32"),
-    "zer": ("sbuf", [128, 32], "float32"),
-    "dk": ("sbuf", [128, 128], "float32"),
-    "dz": ("sbuf", [128, 64], "float32"),
-    "dy": ("sbuf", [128, 320], "float32"),
-    "em": ("sbuf", [128, 592], "bfloat16"),
-    "x0": ("sbuf", [128, 256], "bfloat16"),
-    "x1": ("sbuf", [128, 256], "bfloat16"),
-    "sc0": ("sbuf", [128, 64], "float32"),
-    "sc1": ("sbuf", [128, 64], "float32"),
-    "scy": ("sbuf", [128, 320], "float32"),
-    "scz": ("sbuf", [128, 128], "float32"),
-    "best": ("sbuf", [128, 32], "float32"),
-    "keyi": ("sbuf", [128, 32], "int32"),
-    "leni": ("sbuf", [128, 32], "int32"),
-    "idi": ("sbuf", [128, 32], "int32"),
-    "yl": ("sbuf", [128, 32], "float32"),
-    "yi": ("sbuf", [128, 32], "float32"),
-    "rl": ("dram", [8, 128, 2], "int32"),
-    "idl": ("dram", [8, 128, 64], "bfloat16"),
-}
+SCRATCH = {"rl": ("dram", [8, 128, 2], "int32"), "idl": ("dram", [8, 128, 64], "bfloat16"),
+           "kraw": ("sbuf", [128, 32, 16], "int32"), "kb": ("sbuf", [128, 8, 64], "bfloat16"),
+           "wr": ("sbuf", [128, 4, 128], "bfloat16"), "wi": ("sbuf", [128, 8, 128], "bfloat16"),
+           "pick": ("sbuf", [128, 16, 128], "bfloat16")}
+for _d, _names in (("bfloat16", "win4096 idwin4096 wlb32 halob8 idhi128 idlo128 iom128 ioa128 iob128 blk128 em592 xa256 xb256"),
+                   ("int32", "wl32 halo16 wq32 tidr128 ta128 tz128 tl128 rrow128 pgi1 iop1 ri1 wsi1 keyi32 leni32 idi32"),
+                   ("float32", "rf128 onesf1 rcol1 pg1 iof16 rr1 ws1 rm16 eq8 dd4 da4 db4 ca1 cb1 lowr1 ea1 eb1 bc1 bk6 zer32 dk128 dz64 "
+                               "dy320 sca64 scb64 scy320 scz128 best32 yl32 yi32")):
+    for _n in _names.split():
+        _b = _n.rstrip("0123456789")
+        SCRATCH[_b] = ("sbuf", [128, int(_n[len(_b):])], _d)
 for _k in range(1, 7):
     SCRATCH["l%d" % _k] = ("sbuf", [128, 32], "uint16")
     SCRATCH["y%d" % _k] = ("sbuf", [128, 512], "bfloat16")
 for _k in range(8):
     SCRATCH["p%d" % _k] = ("psum", [128, 512], "float32")
-SEMAPHORES = ["cv", "cs", "ct", "cg", "dl", "dr", "dt", "dhi", "dlo", "drr", "didw", "dyl", "dyi",
-              "r_in", "id_in", "k_in", "r_out", "id_out", "k_out"] + ["dk%d" % k for k in range(4)]
+SEMAPHORES = ["cv", "cs", "ct", "cg", "dl", "dr", "dt", "dhi", "dlo", "drr", "didw", "dyl", "dyi", "go"] + \
+             [a + b for a in ("r", "id", "k") for b in ("_in", "_out")] + ["dk%d" % k for k in range(4)]
 
 
 def rank_program(g, core, T, topo):
@@ -117,122 +64,114 @@ def rank_program(g, core, T, topo):
         return (name + "_in", ne * (N - 1))
 
     done("dr", sy.dma_start(T.rl[me, 0:64, :], T.kid[:, 16:32]), 16)
-    r_own = done("dr", sy.dma_start(T.rl[me, 64:128, :], T.lett[:, 0:16]), 16)
-    tid_ld = done("dt", s.dma_start(T.tidr[0:64, :], T.tid[:]), 16)
-    kid_ld = []
-    for j in range(4):
+    r_own = done("dr", s.dma_start(T.rl[me, 64:128, :], T.lett[:, 0:16]), 16)
+    tid_ld = done("dt", s.dma_start(T.tidr[0:32, :], T.tid[:]), 16)
+
+    def kid_load(queue, j):
         a, gl = j // 2, j % 2
-        kid_ld.append(done("dk%d" % j, (s, sy)[gl].dma_start(T.kraw[:, 16 * gl + 8 * a:16 * gl + 8 * a + 8, :],
-                                                             T.kid[gl::2, 4096 * a:4096 * a + 4096]), 16))
+        return done("dk%d" % j, queue.dma_start(T.kraw[:, 16 * gl + 8 * a:16 * gl + 8 * a + 8, :],
+                                                T.kid[gl::2, 4096 * a:4096 * a + 4096]), 16)
+    kid_ld = [kid_load(s, j) for j in range(3)]
+
+    G(g.iota(T.iop[:], [[0, 1]], 0, 1))
+    io = G(g.iota(T.iom[:], [[16, 8], [0, 16]], 0, 0, allow_small_or_imprecise_dtypes=True))
+    iof = G(g.iota(T.iof[:], [[1, 16]], 0, 0, allow_small_or_imprecise_dtypes=True))
+    idz = V(v.memset(T.idwin[:, 0:512], 0.0))
+    hz = V(v.memset(T.halo[:], 0))
+    V(v.memset(T.onesf[:], 1.0))
+    wait("v", io)
+    V(v.tensor_scalar(T.pgi[:], T.iop[:], 112, None, A.bitwise_and))
+    k0 = V(v.tensor_scalar(T.ri[:], T.iop[:], 15, None, A.bitwise_and))
+
+    wait("v", tid_ld)
+    V(v.tensor_scalar(T.ta[0:32, :], T.tidr[0:32, :], 65280, None, A.bitwise_and))
+    a3 = V(v.tensor_scalar(T.tz[0:32, :], T.tidr[0:32, :], 0, -524288, A.is_equal, A.mult))
+    a4 = V(v.tensor_scalar(T.tl[0:32, :], T.tidr[0:32, :], 255, None, A.bitwise_and))
+    wait("v", k0)
+    V(v.tensor_copy(T.pg[:], T.pgi[:]))
+    k1 = V(v.tensor_copy(T.rr[:], T.ri[:]))
+    wait("v", a3)
+    hi = V(v.tensor_tensor(T.idhi[0:32, :], T.ta[0:32, :], T.tz[0:32, :], A.add))
+    wait("v", a4)
+    lo = V(v.tensor_copy(T.idlo[0:32, :], T.tl[0:32, :]))
+    wait("v", k1, iof)
+    bl = V(v.tensor_scalar(T.blk[:], T.iom[:], T.pg[:, 0:1], None, A.is_equal))
+    rm = V(v.tensor_scalar(T.rm[:], T.iof[:], T.rr[:, 0:1], None, A.is_equal))
+    V(v.tensor_scalar(T.bc[:], T.rr[:], 2.0, 65536.0, A.is_equal, A.mult))
+    k2 = V(v.tensor_scalar(T.wsi[:], T.ri[:], 2, None, A.arith_shift_right))
+    V(v.memset(T.zer[:], 0.0))
+    V(v.memset(T.eq[:], 1.0))
+    wait("y", hi)
+    hi_st = done("dhi", sy.dma_start(T.idl[me, 0:64, :], T.idhi[0:32, :]), 16)
+    wait("y", lo)
+    lo_st = done("dlo", sy.dma_start(T.idl[me, 64:128, :], T.idlo[0:32, :]), 16)
+    kid_ld.append(kid_load(sy, 3))
     lett_ld = done("dl", sy.dma_start(T.wl[:], T.lett[:]), 16)
 
-    o1 = V(v.memset(T.ones[:], 1.0))
-    idz = V(v.memset(T.idwin[:, 0:512], 0.0))
+    wait("g", r_own)
+    r_in = to_all(T.rl[me], "r")
+    io4 = G(g.iota(T.ioa[:], [[16, 8], [0, 4], [1, 4]], 0, 0, allow_small_or_imprecise_dtypes=True))
+    io8 = G(g.iota(T.iob[:], [[16, 8], [0, 2], [1, 8]], 0, 0, allow_small_or_imprecise_dtypes=True))
+    wait("g", hi_st, lo_st)
+    id_in = to_all(T.idl[me], "id")
+
+    wait("s", rm, bl)
+    for r in range(16):
+        pk = S(s.activation(T.pick[:, r, :], T.blk[:], F.Copy, scale=T.rm[:, r:r + 1]))
     wait("s", idz)
     for n in (512, 1024, 2048):
         idz = S(s.activation(T.idwin[:, n:2 * n], T.idwin[:, 0:n], F.Copy))
         wait("s", idz)
-    V(v.memset(T.wr[:], 0.0))
-    V(v.memset(T.onesf[:], 1.0))
-    V(v.memset(T.zer[:], 0.0))
-    V(v.memset(T.eq[:], 1.0))
-    hz = V(v.memset(T.halo[:], 0))
-    G(g.iota(T.iop[:], [[0, 1]], 0, 1))
-    io = G(g.iota(T.iof[:], [[1, 16]], 0, 0, allow_small_or_imprecise_dtypes=True))
-    wait("g", o1)
-    b1 = G(g.affine_select(T.blk1[:], T.ones[:], [[-16, 8], [0, 16]], A.is_ge, 0.0, 0, 1))
-    wait("g", b1)
-    b2 = G(g.affine_select(T.blk[:], T.blk1[:], [[16, 8], [0, 16]], A.is_ge, 0.0, 15, -1))
 
-    wait("v", io)
-    k0 = V(v.tensor_scalar(T.ri[:], T.iop[:], 15, None, A.bitwise_and))
-    wait("v", k0)
-    V(v.tensor_copy(T.rr[:], T.ri[:]))
-    k2 = V(v.tensor_scalar(T.wsi[:], T.ri[:], 2, None, A.arith_shift_right))
-    wait("v", k2)
-    V(v.tensor_scalar(T.rm[:], T.iof[:], T.rr[:, 0:1], None, A.is_equal))
-    V(v.tensor_scalar(T.bc[:], T.rr[:], 2.0, 65536.0, A.is_equal, A.mult))
-    k4 = V(v.tensor_copy(T.ws[:], T.wsi[:]))
-
-    wait("v", tid_ld)
-    V(v.tensor_scalar(T.ta[0:64, :], T.tidr[0:64, :], 65280, None, A.bitwise_and))
-    a3 = V(v.tensor_scalar(T.tz[0:64, :], T.tidr[0:64, :], 0, -524288, A.is_equal, A.mult))
-    a4 = V(v.tensor_scalar(T.tl[0:64, :], T.tidr[0:64, :], 255, None, A.bitwise_and))
-    wait("v", a3)
-    hi = V(v.tensor_tensor(T.idhi[0:64, :], T.ta[0:64, :], T.tz[0:64, :], A.add))
-    wait("v", a4)
-    lo = V(v.tensor_copy(T.idlo[0:64, :], T.tl[0:64, :]))
-    wait("y", hi)
-    hi_st = done("dhi", sy.dma_start(T.idl[me, 0:64, :], T.idhi[0:64, :]), 16)
-    wait("y", lo)
-    lo_st = done("dlo", sy.dma_start(T.idl[me, 64:128, :], T.idlo[0:64, :]), 16)
-
-    wait("g", r_own)
-    r_in = to_all(T.rl[me], "r")
-
-    wait("v", k4, b2)
-
-    def picks(lo, hi):
-        for r in range(lo, hi):
-            pk = V(v.tensor_scalar(T.pick[:, r, :], T.blk[:], T.rm[:, r:r + 1], None, A.mult))
-        return pk
-    for i in range(4):
-        V(v.tensor_copy(T.wr[:, i, i::4], T.blk[:, i::4]))
-    picks(0, 8)
     for j in range(4):
         a, gl = j // 2, j % 2
         wait("v", kid_ld[j])
         kc = V(v.tensor_scalar(T.kb[:, :, 32 * a + 16 * gl:32 * a + 16 * gl + 16],
                                T.kraw[:, 16 * gl + 8 * a:16 * gl + 8 * a + 8, :], 256, None, A.subtract))
+    wait("v", k2)
+    k4 = V(v.tensor_copy(T.ws[:], T.wsi[:]))
+    V(v.tensor_scalar(T.bk[:], T.iof[:, 1:7], T.bc[:, 0:1], None, A.mult))
     wait("v", kc)
     for m in range(8):
         ev = V(v.transpose(T.win[:, 512 * me + m:512 * me + 512:8], T.kb[:, m, :]))
-    wait("g", hi_st, lo_st)
-    id_in = to_all(T.idl[me], "id")
-    wait("g", ev)
+    wait("y", r_in, r_own, hz)
+    done("drr", sy.dma_start(T.rrow[0:8, :], T.rl[:, 0:64, :]), 16)
+    rr_ld = done("drr", sy.dma_start(T.halo[0:128:16, :], T.rl[(me + 1) % N, 64:128, :]), 16)
+    sy.sem_inc(T.sem["go"], 1)
+    total["go"] = 1
+    wait("g", ev, ("go", 1))
     k_in = to_all(T.win[:, 512 * me:512 * me + 512], "k")
 
-    pk = picks(8, 16)
-    wait("v", lett_ld)
+    wait("v", k4, lett_ld)
     wb = V(v.tensor_copy(T.wlb[:], T.wl[:]))
+    V(v.tensor_scalar(T.eq[:, 0:4], T.iof[:, 0:4], T.ws[:, 0:1], None, A.is_equal))
+    c1 = V(v.tensor_scalar(T.lowr[:], T.ws[:], 2.0, None, A.is_lt))
+    V(v.memset(T.dy[:], 0.0))
     wait("t", pk, wb)
     for r in range(16):
         el = P(t.matmul(T.p4[:, r::16], T.pick[:, r, :], T.wlb[:], True, True))
     for r in range(15):
         P(t.matmul(T.p5[:, r:80:16], T.pick[:, r + 1, :], T.wlb[:, 0:5], True, True))
-    V(v.tensor_scalar(T.eq[:, 0:4], T.iof[:, 0:4], T.ws[:, 0:1], None, A.is_equal))
-    c2 = V(v.tensor_scalar(T.wq[:], T.wl[:], 1, None, A.arith_shift_right))
-    V(v.tensor_scalar(T.bk[:], T.iof[:, 1:7], T.bc[:, 0:1], None, A.mult))
-    c1 = V(v.tensor_scalar(T.lowr[:], T.ws[:], 2.0, None, A.is_lt))
-    V(v.memset(T.dy[:], 0.0))
-    wait("v", c2)
-    c3 = V(v.tensor_tensor(T.dd[:], T.eq[:, 0:4], T.eq[:, 1:5], A.subtract))
     wait("v", c1)
-    V(v.tensor_scalar(T.e0[:], T.lowr[:], 2097152.0, 1048576.0, A.mult, A.subtract))
-    V(v.tensor_scalar(T.e1[:], T.lowr[:], -1048576.0, 2097152.0, A.mult, A.subtract))
+    c3 = V(v.tensor_tensor(T.dd[:], T.eq[:, 0:4], T.eq[:, 1:5], A.subtract))
+    c2 = V(v.tensor_scalar(T.wq[:], T.wl[:], 1, None, A.arith_shift_right))
+    V(v.tensor_scalar(T.ea[:], T.lowr[:], 2097152.0, 1048576.0, A.mult, A.subtract))
+    V(v.tensor_scalar(T.eb[:], T.lowr[:], -1048576.0, 2097152.0, A.mult, A.subtract))
     wait("v", c3)
-    V(v.tensor_scalar(T.d1[:], T.dd[:], 16384.0, None, A.mult))
-    V(v.tensor_scalar(T.d2[:], T.dd[:], 1048576.0, None, A.mult))
-    V(v.tensor_scalar(T.c3[:], T.dd[:, 3:4], 16384.0, 7936.0, A.mult, A.subtract))
-    c4 = V(v.tensor_scalar(T.c4[:], T.dd[:, 3:4], 1048576.0, 2097152.0, A.mult, A.subtract))
+    V(v.tensor_scalar(T.da[:], T.dd[:], 16384.0, None, A.mult))
+    c4 = V(v.tensor_scalar(T.ca[:], T.dd[:, 3:4], 16384.0, 7936.0, A.mult, A.subtract))
+    V(v.tensor_scalar(T.db[:], T.dd[:], 1048576.0, None, A.mult))
+    V(v.tensor_scalar(T.cb[:], T.dd[:, 3:4], 1048576.0, 2097152.0, A.mult, A.subtract))
+    wait("v", io4)
+    for i in range(4):
+        V(v.tensor_scalar(T.wr[:, i, :], T.ioa[:], float(-i), T.pg[:, 0:1], A.add, A.is_equal))
     wait("v", c4)
-    for w in range(4):
-        if w < 3:
-            V(v.tensor_scalar(T.dk[:, w::4], T.zer[:], T.d1[:, w:w + 1], None, A.add))
-        V(v.tensor_scalar(T.dz[:, w::4], T.zer[:, 0:16], T.d2[:, w:w + 1] if w < 3 else T.c4[:, 0:1], None, A.add))
-    V(v.tensor_scalar(T.dy[:, 4::10], T.zer[:], T.e0[:, 0:1], None, A.add))
-    V(v.tensor_scalar(T.dy[:, 9::10], T.zer[:], T.e1[:, 0:1], None, A.add))
-    dcon = V(v.tensor_scalar(T.dk[:, 3::4], T.wq[:], 512.0, T.c3[:, 0:1], A.mult, A.add))
+    for w in range(3):
+        V(v.tensor_scalar(T.dk[:, w::4], T.zer[:], T.da[:, w:w + 1], None, A.add))
+    dcon = V(v.tensor_scalar(T.dk[:, 3::4], T.wq[:], 512.0, T.ca[:, 0:1], A.mult, A.add))
     wait("v", el)
     V(v.tensor_scalar(T.em[:, 0:512], T.p4[:], T.rr[:, 0:1], None, A.is_equal))
-    wz = V(v.memset(T.wi[:], 0.0))
-    wait("v", wz)
-    for i in range(8):
-        wi = V(v.tensor_copy(T.wi[:, i, i::8], T.blk[:, i::8]))
 
-    wait("y", r_in, r_own, hz)
-    done("drr", sy.dma_start(T.rrow[0:8, :], T.rl[:, 0:64, :]), 16)
-    rr_ld = done("drr", sy.dma_start(T.halo[0:128:16, :], T.rl[(me + 1) % N, 64:128, :]), 16)
     wait("v", rr_ld)
     rc = V(v.tensor_copy(T.rf[0:8, :], T.rrow[0:8, :]))
     hb = V(v.tensor_copy(T.halob[:], T.halo[:, 0:8]))
@@ -240,10 +179,18 @@ def rank_program(g, core, T, topo):
     rp = P(t.matmul(T.p6[:, 0:1], T.rf[0:8, :], T.onesf[0:8, :], True, True))
     wait("t", hb)
     ex = P(t.matmul(T.p5[:, 15:80:16], T.pick[:, 0, :], T.halob[:, 0:5], True, True))
+    wait("v", io8)
+
+    def id_weights(lo, hi):
+        for i in range(lo, hi):
+            w = V(v.tensor_scalar(T.wi[:, i, :], T.iob[:], float(-i), T.pg[:, 0:1], A.add, A.is_equal))
+        return w
+    id_weights(0, 5)
     wait("v", rp)
     rcol = V(v.tensor_scalar(T.rcol[:], T.p6[:, 0:1], 256.0, None, A.subtract))
     wait("v", ex)
     V(v.tensor_scalar(T.em[:, 512:592], T.p5[:, 0:80], T.rr[:, 0:1], None, A.is_equal))
+    id_weights(5, 7)
     wait("v", rcol)
 
     wait("y", id_in, hi_st, lo_st, idz)
@@ -252,9 +199,8 @@ def rank_program(g, core, T, topo):
         done("didw", sy.dma_start(T.idwin[0:128:16, 512 * j:512 * j + 512], T.idl[j, 0:64, :]), 16)
         done("didw", s.dma_start(T.idwin[1:128:16, 512 * j:512 * j + 512], T.idl[j, 64:128, :]), 16)
     idw = ("didw", total["didw"])
-
-    X = [T.x0, T.x1]
-    SC = [T.sc0, T.sc1]
+    X = [T.xa, T.xb]
+    SC = [T.sca, T.scb]
 
     def kid_sum(h, tok):
         wait("t", tok)
@@ -264,38 +210,51 @@ def rank_program(g, core, T, topo):
 
     xt = [V(v.tensor_scalar(X[h][:], T.em[:, 256 * h:256 * h + 256], T.rcol[:, 0:1], None, A.mult)) for h in range(2)]
     ks = [kid_sum(h, xt[h]) for h in range(2)]
-    yt, ys = {}, {}
+    wi = id_weights(7, 8)
+    V(v.tensor_scalar(T.dy[:, 4::10], T.zer[:], T.ea[:, 0:1], None, A.add))
+    V(v.tensor_scalar(T.dy[:, 9::10], T.zer[:], T.eb[:, 0:1], None, A.add))
+    yt, ys, lt, sc = {}, {}, {}, {}
 
     def id_sum(k, part):
-        if k < 1:
-            return
         wait("t", yt[k, 0], yt[k, 1], wi)
         for i in range(4 * part, 4 * part + 4):
             ys[k] = P(t.matmul(T.p2[:, k - 1:320:5], T.wi[:, i, :], T["y%d" % k][:, i::8], i == 0, i == 7))
 
+    sums = {(3, 0): [(1, 0)], (3, 1): [(1, 1)], (4, 0): [(2, 0)], (4, 1): [(2, 1)], (5, 0): [(3, 0)],
+            (5, 1): [(3, 1), (4, 0), (4, 1)], (6, 0): [(5, 0), (5, 1)]}
+
+    def scan(k, h):
+        wait("v", ks[h], dcon)
+        sc[h] = V(v.tensor_tensor_scan(SC[h][:], T["p%d" % h][:, 0:64], T.dk[:, 64 * h:64 * h + 64], -8192.0, A.max, A.add))
+
+    def node_list(k, h):
+        wait("v", sc[h])
+        lt[h] = V(v.tensor_scalar(T["l%d" % k][:, 16 * h:16 * h + 16], SC[h][:, 3::4], 8192.0, None, A.add))
+
+    def gathers(k, h):
+        off = T["l%d" % k][:, 16 * h:16 * h + 16]
+        y, bias = T["y%d" % k][:, 256 * h:256 * h + 256], T.bk[:, k - 1:k]
+        if k < 6:
+            wait("v", lt[h], k_in, ev)
+            xt[h] = V(v.tensor_tensor(X[h][:], T.win[:].indirect(off), T.em[:, 16 * (k + 16 * h):16 * (k + 16 * h) + 256],
+                                      A.mult))
+            ks[h] = kid_sum(h, xt[h])
+        if k < 6 or h == 0:
+            wait("s", lt[h], idw)
+            yt[k, h] = S(s.activation(y, T.idwin[:].indirect(off), F.Identity, bias=bias))
+        else:
+            wait("v", lt[h], idw)
+            yt[k, h] = V(v.tensor_scalar(y, T.idwin[:].indirect(off), bias, None, A.add))
+        for a, b in sums.get((k, h), []):
+            id_sum(a, b)
+
     for k in range(1, 7):
-        lst = T["l%d" % k]
-        for h in range(2):
-            wait("v", ks[h], dcon)
-            a = V(v.tensor_tensor_scan(SC[h][:], T["p%d" % h][:, 0:64], T.dk[:, 64 * h:64 * h + 64], -8192.0, A.max, A.add))
-            wait("v", a)
-            lt = V(v.tensor_scalar(lst[:, 16 * h:16 * h + 16], SC[h][:, 3::4], 8192.0, None, A.add))
-            off = lst[:, 16 * h:16 * h + 16]
-            y, bias = T["y%d" % k][:, 256 * h:256 * h + 256], T.bk[:, k - 1:k]
-            if k < 6:
-                wait("v", lt, k_in, ev)
-                xt[h] = V(v.tensor_tensor(X[h][:], T.win[:].indirect(off), T.em[:, 16 * (k + 16 * h):16 * (k + 16 * h) + 256],
-                                          A.mult))
-                ks[h] = kid_sum(h, xt[h])
-            if k < 6 or h == 0:
-                wait("s", lt, idw)
-                yt[k, h] = S(s.activation(y, T.idwin[:].indirect(off), F.Identity, bias=bias))
-            else:
-                wait("v", lt, idw)
-                yt[k, h] = V(v.tensor_scalar(y, T.idwin[:].indirect(off), bias, None, A.add))
-            id_sum(k - 2, h)
-    for part in range(2):
-        id_sum(5, part)
+        for f in (scan, node_list, gathers):
+            for h in range(2):
+                f(k, h)
+            if k == 1 and f is node_list:
+                for w in range(4):
+                    V(v.tensor_scalar(T.dz[:, w::4], T.zer[:, 0:16], T.db[:, w:w + 1] if w < 3 else T.cb[:, 0:1], None, A.add))
     for h in range(2):
         wait("t", yt[6, h])
         for i in range(4):
@@ -303,12 +262,12 @@ def rank_program(g, core, T, topo):
 
     wait("v", ys[5])
     a = V(v.tensor_tensor_scan(T.scy[:], T.p2[:, 0:320], T.dy[:], -2097152.0, A.max, A.add))
+    wait("v", ys[6, 0])
+    V(v.tensor_tensor_scan(T.scz[:, 0:64], T.p4[:, 0:64], T.dz[:], -2097152.0, A.max, A.add))
     wait("v", a)
     V(v.tensor_scalar(T.best[:], T.scy[:, 9::10], -2097152.0, None, A.max))
-    for h in range(2):
-        c = slice(64 * h, 64 * h + 64)
-        wait("v", ys[6, h])
-        a = V(v.tensor_tensor_scan(T.scz[:, c], T["p%d" % (4 + h)][:, 0:64], T.dz[:], -2097152.0, A.max, A.add))
+    wait("v", ys[6, 1])
+    a = V(v.tensor_tensor_scan(T.scz[:, 64:128], T.p5[:, 0:64], T.dz[:], -2097152.0, A.max, A.add))
     wait("v", a)
     a = V(v.tensor_tensor(T.keyi[:], T.best[:], T.scz[:, 3::4], A.max))
     wait("v", a)

@@ -19,7 +19,7 @@ for _k in range(1, 7):
 for _k in range(8):
     SCRATCH["p%d" % _k] = ("psum", [128, 512], "float32")
 SEMAPHORES = ["cv", "cs", "ct", "cg", "dl", "dr", "dt", "dhi", "dlo", "drr", "didw", "dyl", "dyi", "go"] + \
-             [a + b for a in ("r", "id", "k") for b in ("_in", "_out")] + ["dk%d" % k for k in range(4)]
+             [a + b for a in ("r", "id", "x", "k", "f") for b in ("_in", "_out")] + ["dk%d" % k for k in range(4)]
 
 
 def rank_program(g, core, T, topo):
@@ -46,74 +46,77 @@ def rank_program(g, core, T, topo):
     def G(inst): return done("cg", inst)
     v, s, t, sy = g.vector, g.scalar, g.tensor, g.sync
     peers = [T.cores[(me + d) % N] for d in range(1, N)]
-    mask = topo.mask(core, peers[0])
-    for c in peers:
-        mask = mask & topo.mask(core, c)
-    ne = bin(mask).count("1")
+    own = [c for c in T.cores if topo.die(c) == topo.die(core)]
+    other = [c for c in T.cores if topo.die(c) != topo.die(core)]
+    at = own.index(core)
+    partner = other[at]
+    near = [own[(at + d) % len(own)] for d in range(1, len(own))]
 
     def dst(c):
         a = topo.addr(c)
         return DstId(rid=a[0], pnc=a[1])
 
-    def to_all(src, name):
-        g.remote_dma_fused([RemoteDMATransfer(dst_ids=[dst(c) for c in peers], dma_engine_mask=mask,
-                                              remote_sem=T.sem[name + "_in"], srcs=[src], dsts=[src for c in peers])],
+    def send(src, name, to):
+        mask = topo.mask(core, to[0])
+        for c in to:
+            mask = mask & topo.mask(core, c)
+        ne = bin(mask).count("1")
+        g.remote_dma_fused([RemoteDMATransfer(dst_ids=[dst(c) for c in to], dma_engine_mask=mask,
+                                              remote_sem=T.sem[name + "_in"], srcs=[src], dsts=[src for c in to])],
                            local_sem=T.sem[name + "_out"])
         total[name + "_out"] = ne
-        total[name + "_in"] = ne * (N - 1)
-        return (name + "_in", ne * (N - 1))
+        total[name + "_in"] = ne * len(to)
+        return (name + "_in", ne * len(to))
 
     done("dr", sy.dma_start(T.rl[me, 0:64, :], T.kid[:, 16:32]), 16)
     r_own = done("dr", s.dma_start(T.rl[me, 64:128, :], T.lett[:, 0:16]), 16)
     tid_ld = done("dt", s.dma_start(T.tidr[0:32, :], T.tid[:]), 16)
-
-    def kid_load(queue, j):
+    kid_ld = []
+    for j in range(4):
         a, gl = j // 2, j % 2
-        return done("dk%d" % j, queue.dma_start(T.kraw[:, 16 * gl + 8 * a:16 * gl + 8 * a + 8, :],
-                                                T.kid[gl::2, 4096 * a:4096 * a + 4096]), 16)
-    kid_ld = [kid_load(s, j) for j in range(3)]
+        kid_ld.append(done("dk%d" % j, s.dma_start(T.kraw[:, 16 * gl + 8 * a:16 * gl + 8 * a + 8, :],
+                                                   T.kid[gl::2, 4096 * a:4096 * a + 4096]), 16))
+    lett_ld = done("dl", s.dma_start(T.wl[:], T.lett[:]), 16)
 
-    G(g.iota(T.iop[:], [[0, 1]], 0, 1))
-    io = G(g.iota(T.iom[:], [[16, 8], [0, 16]], 0, 0, allow_small_or_imprecise_dtypes=True))
+    ip = G(g.iota(T.iop[:], [[0, 1]], 0, 1))
+    G(g.iota(T.iom[:], [[16, 8], [0, 16]], 0, 0, allow_small_or_imprecise_dtypes=True))
     iof = G(g.iota(T.iof[:], [[1, 16]], 0, 0, allow_small_or_imprecise_dtypes=True))
-    idz = V(v.memset(T.idwin[:, 0:512], 0.0))
     hz = V(v.memset(T.halo[:], 0))
     V(v.memset(T.onesf[:], 1.0))
-    wait("v", io)
+    wait("v", ip)
     V(v.tensor_scalar(T.pgi[:], T.iop[:], 112, None, A.bitwise_and))
     k0 = V(v.tensor_scalar(T.ri[:], T.iop[:], 15, None, A.bitwise_and))
+    idz = V(v.memset(T.idwin[:, 0:512], 0.0))
+    wait("v", k0)
+    V(v.tensor_copy(T.pg[:], T.pgi[:]))
+    k1 = V(v.tensor_copy(T.rr[:], T.ri[:]))
+    k2 = V(v.tensor_scalar(T.wsi[:], T.ri[:], 2, None, A.arith_shift_right))
+    V(v.memset(T.zer[:], 0.0))
+    wait("v", k1, iof)
+    bl = V(v.tensor_scalar(T.blk[:], T.iom[:], T.pg[:, 0:1], None, A.is_equal))
+    rm = V(v.tensor_scalar(T.rm[:], T.iof[:], T.rr[:, 0:1], None, A.is_equal))
 
     wait("v", tid_ld)
     V(v.tensor_scalar(T.ta[0:32, :], T.tidr[0:32, :], 65280, None, A.bitwise_and))
     a3 = V(v.tensor_scalar(T.tz[0:32, :], T.tidr[0:32, :], 0, -524288, A.is_equal, A.mult))
     a4 = V(v.tensor_scalar(T.tl[0:32, :], T.tidr[0:32, :], 255, None, A.bitwise_and))
-    wait("v", k0)
-    V(v.tensor_copy(T.pg[:], T.pgi[:]))
-    k1 = V(v.tensor_copy(T.rr[:], T.ri[:]))
+    k3 = V(v.tensor_scalar(T.bc[:], T.rr[:], 2.0, 65536.0, A.is_equal, A.mult))
     wait("v", a3)
     hi = V(v.tensor_tensor(T.idhi[0:32, :], T.ta[0:32, :], T.tz[0:32, :], A.add))
     wait("v", a4)
     lo = V(v.tensor_copy(T.idlo[0:32, :], T.tl[0:32, :]))
-    wait("v", k1, iof)
-    bl = V(v.tensor_scalar(T.blk[:], T.iom[:], T.pg[:, 0:1], None, A.is_equal))
-    rm = V(v.tensor_scalar(T.rm[:], T.iof[:], T.rr[:, 0:1], None, A.is_equal))
-    V(v.tensor_scalar(T.bc[:], T.rr[:], 2.0, 65536.0, A.is_equal, A.mult))
-    k2 = V(v.tensor_scalar(T.wsi[:], T.ri[:], 2, None, A.arith_shift_right))
-    V(v.memset(T.zer[:], 0.0))
     V(v.memset(T.eq[:], 1.0))
     wait("y", hi)
     hi_st = done("dhi", sy.dma_start(T.idl[me, 0:64, :], T.idhi[0:32, :]), 16)
     wait("y", lo)
     lo_st = done("dlo", sy.dma_start(T.idl[me, 64:128, :], T.idlo[0:32, :]), 16)
-    kid_ld.append(kid_load(sy, 3))
-    lett_ld = done("dl", sy.dma_start(T.wl[:], T.lett[:]), 16)
 
     wait("g", r_own)
-    r_in = to_all(T.rl[me], "r")
+    r_in = send(T.rl[me], "r", peers)
     io4 = G(g.iota(T.ioa[:], [[16, 8], [0, 4], [1, 4]], 0, 0, allow_small_or_imprecise_dtypes=True))
     io8 = G(g.iota(T.iob[:], [[16, 8], [0, 2], [1, 8]], 0, 0, allow_small_or_imprecise_dtypes=True))
     wait("g", hi_st, lo_st)
-    id_in = to_all(T.idl[me], "id")
+    id_in = send(T.idl[me], "id", peers)
 
     wait("s", rm, bl)
     for r in range(16):
@@ -128,7 +131,7 @@ def rank_program(g, core, T, topo):
         wait("v", kid_ld[j])
         kc = V(v.tensor_scalar(T.kb[:, :, 32 * a + 16 * gl:32 * a + 16 * gl + 16],
                                T.kraw[:, 16 * gl + 8 * a:16 * gl + 8 * a + 8, :], 256, None, A.subtract))
-    wait("v", k2)
+    wait("v", k2, k3)
     k4 = V(v.tensor_copy(T.ws[:], T.wsi[:]))
     V(v.tensor_scalar(T.bk[:], T.iof[:, 1:7], T.bc[:, 0:1], None, A.mult))
     wait("v", kc)
@@ -139,8 +142,13 @@ def rank_program(g, core, T, topo):
     rr_ld = done("drr", sy.dma_start(T.halo[0:128:16, :], T.rl[(me + 1) % N, 64:128, :]), 16)
     sy.sem_inc(T.sem["go"], 1)
     total["go"] = 1
-    wait("g", ev, ("go", 1))
-    k_in = to_all(T.win[:, 512 * me:512 * me + 512], "k")
+    wait("g", ev)
+    x_in = send(T.win[:, 512 * me:512 * me + 512], "x", [partner])
+    wait("g", ("go", 1))
+    k_in = send(T.win[:, 512 * me:512 * me + 512], "k", near)
+    wait("g", x_in)
+    pr = T.rank_of(partner)
+    f_in = send(T.win[:, 512 * pr:512 * pr + 512], "f", near)
 
     wait("v", k4, lett_ld)
     wb = V(v.tensor_copy(T.wlb[:], T.wl[:]))
@@ -235,7 +243,7 @@ def rank_program(g, core, T, topo):
         off = T["l%d" % k][:, 16 * h:16 * h + 16]
         y, bias = T["y%d" % k][:, 256 * h:256 * h + 256], T.bk[:, k - 1:k]
         if k < 6:
-            wait("v", lt[h], k_in, ev)
+            wait("v", lt[h], x_in, k_in, f_in, ev)
             xt[h] = V(v.tensor_tensor(X[h][:], T.win[:].indirect(off), T.em[:, 16 * (k + 16 * h):16 * (k + 16 * h) + 256],
                                       A.mult))
             ks[h] = kid_sum(h, xt[h])

@@ -1,25 +1,29 @@
 from concourse.bass import DstId, RemoteDMATransfer
-from concourse.mybir import AluOpType as A, ActivationFunctionType as F
+from concourse.mybir import AluOpType as A, ActivationFunctionType as F, AxisListType
 
 N = 8
 SCRATCH = {"rl": ("dram", [8, 128, 2], "int32"), "idl": ("dram", [8, 128, 64], "bfloat16"),
            "kraw": ("sbuf", [128, 32, 16], "int32"), "kb": ("sbuf", [128, 8, 64], "bfloat16"),
            "wr": ("sbuf", [128, 4, 128], "bfloat16"), "wi": ("sbuf", [128, 8, 128], "bfloat16"),
            "pick": ("sbuf", [128, 16, 128], "bfloat16")}
-for _d, _names in (("bfloat16", "win4096 idwin4096 wlb32 halob8 idhi128 idlo128 iom128 ioa128 iob128 blk128 em592 xa256 xb256"),
-                   ("int32", "wl32 halo16 wq32 tidr128 ta128 tz128 tl128 rrow128 pgi1 iop1 ri1 wsi1 keyi32 leni32 idi32"),
-                   ("float32", "rf128 onesf1 rcol1 pg1 iof16 rr1 ws1 rm16 eq8 dd4 da4 db4 ca1 cb1 lowr1 ea1 eb1 bc1 bk6 zer32 dk128 dz64 "
-                               "dy320 sca64 scb64 scy320 scz128 best32 yl32 yi32")):
+for _d, _names in (("bfloat16", "win4096 idwin4096 pw384 pf16 bs8 idp384 wlb32 halob8 idhi128 idlo128 iom128 ioa128 iob128 blk128 "
+                                "em592 xa256 xb256"),
+                   ("int32", "wl32 halo32 wa32 wb32 wd32 we32 wf32 wg32 wh32 wj32 wq32 tidr128 ta128 tz128 tl128 pgi1 iop1 ri1 "
+                             "wsi1 keyi32 leni32 idi32"),
+                   ("float32", "lp24 ctmp16 cnext1 pg1 iof16 rr1 ws1 rm16 eq8 dd4 da4 db4 ca1 cb1 lowr1 ea1 eb1 bc1 bk6 "
+                               "zer32 dk128 dz64 dy320 sca64 scb64 scy320 scz128 best32 yl32 yi32"),
+                   ("uint16", "lone2 ltwo2 lpre24 lc32 lq32")):
     for _n in _names.split():
         _b = _n.rstrip("0123456789")
         SCRATCH[_b] = ("sbuf", [128, int(_n[len(_b):])], _d)
 for _k in range(1, 7):
-    SCRATCH["l%d" % _k] = ("sbuf", [128, 32], "uint16")
+    if _k > 2:
+        SCRATCH["l%d" % _k] = ("sbuf", [128, 32], "uint16")
     SCRATCH["y%d" % _k] = ("sbuf", [128, 512], "bfloat16")
-for _k in range(8):
+for _k in (0, 1, 2, 4, 5):
     SCRATCH["p%d" % _k] = ("psum", [128, 512], "float32")
-SEMAPHORES = ["cv", "cs", "ct", "cg", "dl", "dr", "dt", "dhi", "dlo", "drr", "didw", "dyl", "dyi", "go"] + \
-             [a + b for a in ("r", "id", "x", "k", "f") for b in ("_in", "_out")] + ["dk%d" % k for k in range(4)]
+SEMAPHORES = ["cv", "cs", "ct", "cg", "dl", "dr", "dt", "dhi", "dlo", "drr", "didw", "dyl", "dyi"] + \
+             [a + b for a in ("r", "id", "x", "p", "n", "k") for b in ("_in", "_out")] + ["dk%d" % k for k in range(4)]
 
 
 def rank_program(g, core, T, topo):
@@ -45,12 +49,12 @@ def rank_program(g, core, T, topo):
     def P(inst): return done("ct", inst)
     def G(inst): return done("cg", inst)
     v, s, t, sy = g.vector, g.scalar, g.tensor, g.sync
+    H, NB = N // 2, 48
     peers = [T.cores[(me + d) % N] for d in range(1, N)]
-    own = [c for c in T.cores if topo.die(c) == topo.die(core)]
-    other = [c for c in T.cores if topo.die(c) != topo.die(core)]
-    at = own.index(core)
-    partner = other[at]
-    near = [own[(at + d) % len(own)] for d in range(1, len(own))]
+    pos = [2 * (j % H) + j // H for j in range(N)]
+    at, partner = me % H, T.cores[(me + H) % N]
+    near = [T.cores[me - at + (at + d) % H] for d in range(1, H)]
+    wb0, pb0 = 512 * pos[me], NB * pos[me]
 
     def dst(c):
         a = topo.addr(c)
@@ -68,25 +72,24 @@ def rank_program(g, core, T, topo):
         total[name + "_in"] = ne * len(to)
         return (name + "_in", ne * len(to))
 
-    done("dr", sy.dma_start(T.rl[me, 0:64, :], T.kid[:, 16:32]), 16)
-    r_own = done("dr", s.dma_start(T.rl[me, 64:128, :], T.lett[:, 0:16]), 16)
+    r_own = done("dr", sy.dma_start(T.rl[me], T.lett[:, 0:32]), 16)
     tid_ld = done("dt", s.dma_start(T.tidr[0:32, :], T.tid[:]), 16)
     kid_ld = []
     for j in range(4):
         a, gl = j // 2, j % 2
-        kid_ld.append(done("dk%d" % j, s.dma_start(T.kraw[:, 16 * gl + 8 * a:16 * gl + 8 * a + 8, :],
-                                                   T.kid[gl::2, 4096 * a:4096 * a + 4096]), 16))
-    lett_ld = done("dl", s.dma_start(T.wl[:], T.lett[:]), 16)
+        kid_ld.append(done("dk%d" % j, (sy, s)[gl].dma_start(T.kraw[:, 16 * gl + 8 * a:16 * gl + 8 * a + 8, :],
+                                                             T.kid[gl::2, 4096 * a:4096 * a + 4096]), 16))
+    lett_ld = done("dl", sy.dma_start(T.wl[:], T.lett[:]), 16)
 
     ip = G(g.iota(T.iop[:], [[0, 1]], 0, 1))
     G(g.iota(T.iom[:], [[16, 8], [0, 16]], 0, 0, allow_small_or_imprecise_dtypes=True))
     iof = G(g.iota(T.iof[:], [[1, 16]], 0, 0, allow_small_or_imprecise_dtypes=True))
     hz = V(v.memset(T.halo[:], 0))
-    V(v.memset(T.onesf[:], 1.0))
+    V(v.memset(T.pw[:, pb0 + 32:pb0 + NB], 0.0))
     wait("v", ip)
     V(v.tensor_scalar(T.pgi[:], T.iop[:], 112, None, A.bitwise_and))
     k0 = V(v.tensor_scalar(T.ri[:], T.iop[:], 15, None, A.bitwise_and))
-    idz = V(v.memset(T.idwin[:, 0:512], 0.0))
+    idz = V(v.memset(T.idwin[:, 0:1024], 0.0))
     wait("v", k0)
     V(v.tensor_copy(T.pg[:], T.pgi[:]))
     k1 = V(v.tensor_copy(T.rr[:], T.ri[:]))
@@ -112,9 +115,10 @@ def rank_program(g, core, T, topo):
     lo_st = done("dlo", sy.dma_start(T.idl[me, 64:128, :], T.idlo[0:32, :]), 16)
 
     wait("g", r_own)
-    r_in = send(T.rl[me], "r", peers)
+    r_in = send(T.rl[me], "r", [T.cores[(me - 1) % N]])
     io4 = G(g.iota(T.ioa[:], [[16, 8], [0, 4], [1, 4]], 0, 0, allow_small_or_imprecise_dtypes=True))
     io8 = G(g.iota(T.iob[:], [[16, 8], [0, 2], [1, 8]], 0, 0, allow_small_or_imprecise_dtypes=True))
+    bs = G(g.iota(T.bs[:], [[512, 8]], 256, 0, allow_small_or_imprecise_dtypes=True))
     wait("g", hi_st, lo_st)
     id_in = send(T.idl[me], "id", peers)
 
@@ -122,7 +126,7 @@ def rank_program(g, core, T, topo):
     for r in range(16):
         pk = S(s.activation(T.pick[:, r, :], T.blk[:], F.Copy, scale=T.rm[:, r:r + 1]))
     wait("s", idz)
-    for n in (512, 1024, 2048):
+    for n in (1024, 2048):
         idz = S(s.activation(T.idwin[:, n:2 * n], T.idwin[:, 0:n], F.Copy))
         wait("s", idz)
 
@@ -135,77 +139,96 @@ def rank_program(g, core, T, topo):
     k4 = V(v.tensor_copy(T.ws[:], T.wsi[:]))
     V(v.tensor_scalar(T.bk[:], T.iof[:, 1:7], T.bc[:, 0:1], None, A.mult))
     wait("v", kc)
-    for m in range(8):
-        ev = V(v.transpose(T.win[:, 512 * me + m:512 * me + 512:8], T.kb[:, m, :]))
-    wait("y", r_in, r_own, hz)
-    done("drr", sy.dma_start(T.rrow[0:8, :], T.rl[:, 0:64, :]), 16)
-    rr_ld = done("drr", sy.dma_start(T.halo[0:128:16, :], T.rl[(me + 1) % N, 64:128, :]), 16)
-    sy.sem_inc(T.sem["go"], 1)
-    total["go"] = 1
+    for m in (1, 0, 2, 3, 4, 5, 6, 7):
+        ev = V(v.transpose(T.win[:, wb0 + m:wb0 + 512:8], T.kb[:, m, :]))
+        if m == 1:
+            root = ev
+        if m == 6:
+            wait("v", root)
+            l1 = V(v.tensor_scalar(T.lone[:, 0:1], T.win[:, wb0 + 1:wb0 + 2], 256, None, A.add))
+            V(v.tensor_copy(T.pw[:, pb0 + 34:pb0 + 35], T.win[:, wb0 + 1:wb0 + 2]))
     wait("g", ev)
-    x_in = send(T.win[:, 512 * me:512 * me + 512], "x", [partner])
-    wait("g", ("go", 1))
-    k_in = send(T.win[:, 512 * me:512 * me + 512], "k", near)
-    wait("g", x_in)
-    pr = T.rank_of(partner)
-    f_in = send(T.win[:, 512 * pr:512 * pr + 512], "f", near)
+    x_in = send(T.win[:, wb0:wb0 + 512], "x", [partner])
 
+    wait("v", ev, l1)
+    g1 = V(v.tensor_copy(T.pf[:], T.win[:, wb0:wb0 + 512].indirect(T.lone[:, 0:1])))
     wait("v", k4, lett_ld)
     wb = V(v.tensor_copy(T.wlb[:], T.wl[:]))
-    V(v.tensor_scalar(T.eq[:, 0:4], T.iof[:, 0:4], T.ws[:, 0:1], None, A.is_equal))
-    c1 = V(v.tensor_scalar(T.lowr[:], T.ws[:], 2.0, None, A.is_lt))
-    V(v.memset(T.dy[:], 0.0))
+    wait("v", g1)
+    l2 = V(v.tensor_scalar(T.ltwo[:], T.pf[:, 2 * me:2 * me + 2], 256, None, A.add))
+    V(v.tensor_copy(T.pw[:, pb0 + 32:pb0 + 34], T.pf[:, 2 * me:2 * me + 2]))
+    wait("v", l2)
+    p3 = V(v.tensor_copy(T.pw[:, pb0:pb0 + 32], T.win[:, wb0:wb0 + 512].indirect(T.ltwo[:])))
+    wait("g", p3)
+    p_in = send(T.pw[:, pb0:pb0 + NB], "p", [partner])
+    wait("g", p_in)
+    n_in = send(T.pw[:, 2 * NB * at:2 * NB * at + 2 * NB], "n", near)
+    wait("g", x_in)
+    k_in = send(T.win[:, 1024 * at:1024 * at + 1024], "k", near)
+    wait("y", r_in, hz)
+    rr_ld = done("drr", sy.dma_start(T.halo[0:128:16, :], T.rl[(me + 1) % N]), 16)
+
     wait("t", pk, wb)
     for r in range(16):
-        el = P(t.matmul(T.p4[:, r::16], T.pick[:, r, :], T.wlb[:], True, True))
+        P(t.matmul(T.p4[:, r::16], T.pick[:, r, :], T.wlb[:], True, True))
     for r in range(15):
         P(t.matmul(T.p5[:, r:80:16], T.pick[:, r + 1, :], T.wlb[:, 0:5], True, True))
+    V(v.tensor_scalar(T.wa[:], T.wl[:], 6, None, A.bitwise_and))
+    c2 = V(v.tensor_scalar(T.wb[:], T.wl[:], 3, None, A.arith_shift_right))
+    c5 = V(v.tensor_scalar(T.wd[:], T.wl[:], 1, None, A.bitwise_and))
+    c1 = V(v.tensor_scalar(T.eq[:, 0:4], T.iof[:, 0:4], T.ws[:, 0:1], None, A.is_equal))
+    wait("v", c2)
+    c2 = V(v.tensor_tensor(T.wq[:], T.wa[:], T.wb[:], A.add))
     wait("v", c1)
     c3 = V(v.tensor_tensor(T.dd[:], T.eq[:, 0:4], T.eq[:, 1:5], A.subtract))
-    c2 = V(v.tensor_scalar(T.wq[:], T.wl[:], 1, None, A.arith_shift_right))
-    V(v.tensor_scalar(T.ea[:], T.lowr[:], 2097152.0, 1048576.0, A.mult, A.subtract))
-    V(v.tensor_scalar(T.eb[:], T.lowr[:], -1048576.0, 2097152.0, A.mult, A.subtract))
+    c5 = V(v.tensor_scalar(T.we[:], T.wd[:], 16, None, A.mult))
     wait("v", c3)
     V(v.tensor_scalar(T.da[:], T.dd[:], 16384.0, None, A.mult))
     c4 = V(v.tensor_scalar(T.ca[:], T.dd[:, 3:4], 16384.0, 7936.0, A.mult, A.subtract))
-    V(v.tensor_scalar(T.db[:], T.dd[:], 1048576.0, None, A.mult))
-    V(v.tensor_scalar(T.cb[:], T.dd[:, 3:4], 1048576.0, 2097152.0, A.mult, A.subtract))
+    wait("v", c2, c5)
+    c7 = V(v.tensor_scalar(T.wf[:], T.wq[:], NB, None, A.mult))
+    V(v.tensor_tensor(T.wg[:, 0:31], T.we[:, 0:31], T.wl[:, 1:32], A.add))
+    wait("v", rr_ld)
+    hb = V(v.tensor_copy(T.halob[:], T.halo[:, 0:8]))
+    wait("t", hb)
+    ex = P(t.matmul(T.p5[:, 15:80:16], T.pick[:, 0, :], T.halob[:, 0:5], True, True))
+    wait("v", c7)
+    c7 = V(v.tensor_tensor(T.wj[:], T.wf[:], T.wl[:], A.add))
     wait("v", io4)
     for i in range(4):
         V(v.tensor_scalar(T.wr[:, i, :], T.ioa[:], float(-i), T.pg[:, 0:1], A.add, A.is_equal))
     wait("v", c4)
     for w in range(3):
         V(v.tensor_scalar(T.dk[:, w::4], T.zer[:], T.da[:, w:w + 1], None, A.add))
+    wait("v", c7)
+    V(v.tensor_copy(T.lc[:], T.wj[:]))
     dcon = V(v.tensor_scalar(T.dk[:, 3::4], T.wq[:], 512.0, T.ca[:, 0:1], A.mult, A.add))
-    wait("v", el)
-    V(v.tensor_scalar(T.em[:, 0:512], T.p4[:], T.rr[:, 0:1], None, A.is_equal))
-
-    wait("v", rr_ld)
-    rc = V(v.tensor_copy(T.rf[0:8, :], T.rrow[0:8, :]))
-    hb = V(v.tensor_copy(T.halob[:], T.halo[:, 0:8]))
-    wait("t", rc)
-    rp = P(t.matmul(T.p6[:, 0:1], T.rf[0:8, :], T.onesf[0:8, :], True, True))
-    wait("t", hb)
-    ex = P(t.matmul(T.p5[:, 15:80:16], T.pick[:, 0, :], T.halob[:, 0:5], True, True))
-    wait("v", io8)
-
-    def id_weights(lo, hi):
-        for i in range(lo, hi):
-            w = V(v.tensor_scalar(T.wi[:, i, :], T.iob[:], float(-i), T.pg[:, 0:1], A.add, A.is_equal))
-        return w
-    id_weights(0, 5)
-    wait("v", rp)
-    rcol = V(v.tensor_scalar(T.rcol[:], T.p6[:, 0:1], 256.0, None, A.subtract))
     wait("v", ex)
+    c6 = V(v.tensor_tensor(T.ctmp[:], T.p5[:, 0:16], T.rm[:], A.mult))
     V(v.tensor_scalar(T.em[:, 512:592], T.p5[:, 0:80], T.rr[:, 0:1], None, A.is_equal))
-    id_weights(5, 7)
-    wait("v", rcol)
+    wait("v", c6)
+    c6 = V(v.tensor_reduce(T.cnext[:], T.ctmp[:], AxisListType.X, A.add))
+    V(v.tensor_scalar(T.em[:, 0:512], T.p4[:], T.rr[:, 0:1], None, A.is_equal))
+    wait("v", c6, io8)
+
+    def id_weight(i):
+        return V(v.tensor_scalar(T.wi[:, i, :], T.iob[:], float(-i), T.pg[:, 0:1], A.add, A.is_equal))
+    c6 = V(v.tensor_scalar(T.wg[:, 31:32], T.we[:, 31:32], T.cnext[:, 0:1], None, A.add))
+    id_weight(0)
+    wait("v", c6)
+    c6 = V(v.tensor_tensor(T.wh[:], T.wf[:], T.wg[:], A.add))
+    id_weight(1)
+    wait("v", c6)
+    lq = V(v.tensor_copy(T.lq[:], T.wh[:]))
+    for i in range(2, 8):
+        wi = id_weight(i)
 
     wait("y", id_in, hi_st, lo_st, idz)
     wait("s", id_in, hi_st, lo_st, idz)
     for j in range(N):
-        done("didw", sy.dma_start(T.idwin[0:128:16, 512 * j:512 * j + 512], T.idl[j, 0:64, :]), 16)
-        done("didw", s.dma_start(T.idwin[1:128:16, 512 * j:512 * j + 512], T.idl[j, 64:128, :]), 16)
+        b = 512 * pos[j]
+        done("didw", sy.dma_start(T.idwin[0:128:16, b:b + 512], T.idl[j, 0:64, :]), 16)
+        done("didw", s.dma_start(T.idwin[1:128:16, b:b + 512], T.idl[j, 64:128, :]), 16)
     idw = ("didw", total["didw"])
     X = [T.xa, T.xb]
     SC = [T.sca, T.scb]
@@ -216,12 +239,7 @@ def rank_program(g, core, T, topo):
             r = P(t.matmul(T["p%d" % h][:, 0:64], T.wr[:, i, :], X[h][:, i::4], i == 0, i == 3))
         return r
 
-    xt = [V(v.tensor_scalar(X[h][:], T.em[:, 256 * h:256 * h + 256], T.rcol[:, 0:1], None, A.mult)) for h in range(2)]
-    ks = [kid_sum(h, xt[h]) for h in range(2)]
-    wi = id_weights(7, 8)
-    V(v.tensor_scalar(T.dy[:, 4::10], T.zer[:], T.ea[:, 0:1], None, A.add))
-    V(v.tensor_scalar(T.dy[:, 9::10], T.zer[:], T.eb[:, 0:1], None, A.add))
-    yt, ys, lt, sc = {}, {}, {}, {}
+    yt, ys, lt, sc, xt, ks = {}, {}, {}, {}, {}, {}
 
     def id_sum(k, part):
         wait("t", yt[k, 0], yt[k, 1], wi)
@@ -243,7 +261,7 @@ def rank_program(g, core, T, topo):
         off = T["l%d" % k][:, 16 * h:16 * h + 16]
         y, bias = T["y%d" % k][:, 256 * h:256 * h + 256], T.bk[:, k - 1:k]
         if k < 6:
-            wait("v", lt[h], x_in, k_in, f_in, ev)
+            wait("v", lt[h], x_in, k_in, ev)
             xt[h] = V(v.tensor_tensor(X[h][:], T.win[:].indirect(off), T.em[:, 16 * (k + 16 * h):16 * (k + 16 * h) + 256],
                                       A.mult))
             ks[h] = kid_sum(h, xt[h])
@@ -256,13 +274,51 @@ def rank_program(g, core, T, topo):
         for a, b in sums.get((k, h), []):
             id_sum(a, b)
 
-    for k in range(1, 7):
-        for f in (scan, node_list, gathers):
+    for h in range(2):
+        wait("v", lq, p3, p_in, n_in)
+        xt[h] = V(v.tensor_tensor(X[h][:], T.pw[:].indirect(T.lq[:, 16 * h:16 * h + 16]),
+                                  T.em[:, 16 * (2 + 16 * h):16 * (2 + 16 * h) + 256], A.mult))
+        ks[h] = kid_sum(h, xt[h])
+    wait("v", bs)
+    for i in range(3):
+        b = V(v.tensor_tensor(T.lp[:, i::3], T.pw[:, 32 + i::NB], T.bs[:], A.add))
+    wait("v", b)
+    lp = V(v.tensor_copy(T.lpre[:], T.lp[:]))
+    wait("s", lp, idw)
+    idp = S(s.activation(T.idp[:], T.idwin[:].indirect(T.lpre[:]), F.Copy))
+    wait("s", idp)
+    for h in range(2):
+        yt[1, h] = S(s.activation(T.y1[:, 256 * h:256 * h + 256], T.idp[:, 32:384].indirect(T.lc[:, 16 * h:16 * h + 16]),
+                                  F.Identity, bias=T.bk[:, 0:1]))
+    for h in range(2):
+        yt[2, h] = S(s.activation(T.y2[:, 256 * h:256 * h + 256], T.idp[:].indirect(T.lq[:, 16 * h:16 * h + 16]),
+                                  F.Identity, bias=T.bk[:, 1:2]))
+
+    def gap(k):
+        if k == 3:
+            V(v.tensor_scalar(T.db[:], T.dd[:], 1048576.0, None, A.mult))
+            V(v.tensor_scalar(T.cb[:], T.dd[:, 3:4], 1048576.0, 2097152.0, A.mult, A.subtract))
+            return V(v.tensor_scalar(T.lowr[:], T.ws[:], 2.0, None, A.is_lt))
+        if k == 4:
+            V(v.tensor_scalar(T.ea[:], T.lowr[:], 2097152.0, 1048576.0, A.mult, A.subtract))
+            V(v.tensor_scalar(T.eb[:], T.lowr[:], -1048576.0, 2097152.0, A.mult, A.subtract))
+            return V(v.memset(T.dy[:], 0.0))
+        if k == 5:
+            for w in range(4):
+                V(v.tensor_scalar(T.dz[:, w::4], T.zer[:, 0:16], T.db[:, w:w + 1] if w < 3 else T.cb[:, 0:1], None, A.add))
+        if k == 6:
+            V(v.tensor_scalar(T.dy[:, 4::10], T.zer[:], T.ea[:, 0:1], None, A.add))
+            return V(v.tensor_scalar(T.dy[:, 9::10], T.zer[:], T.eb[:, 0:1], None, A.add))
+
+    made = None
+    for k in range(3, 7):
+        scan(k, 0)
+        wait("v", made)
+        made = gap(k) or made
+        scan(k, 1)
+        for f in (node_list, gathers):
             for h in range(2):
                 f(k, h)
-            if k == 1 and f is node_list:
-                for w in range(4):
-                    V(v.tensor_scalar(T.dz[:, w::4], T.zer[:, 0:16], T.db[:, w:w + 1] if w < 3 else T.cb[:, 0:1], None, A.add))
     for h in range(2):
         wait("t", yt[6, h])
         for i in range(4):

@@ -1,17 +1,16 @@
 from concourse.bass import DstId, RemoteDMATransfer
-from concourse.mybir import AluOpType as A, ActivationFunctionType as F, AxisListType
+from concourse.mybir import AluOpType as A, ActivationFunctionType as F
 
 N = 8
 SCRATCH = {"rl": ("dram", [8, 128, 2], "int32"), "idl": ("dram", [8, 128, 64], "bfloat16"),
            "kraw": ("sbuf", [128, 32, 16], "int32"), "kb": ("sbuf", [128, 8, 64], "bfloat16"),
-           "wr": ("sbuf", [128, 4, 128], "bfloat16"), "wi": ("sbuf", [128, 8, 128], "bfloat16"),
-           "pick": ("sbuf", [128, 16, 128], "bfloat16")}
-for _d, _names in (("bfloat16", "win4096 idwin4096 pw384 pf16 bs8 idp384 wlb32 halob8 idhi128 idlo128 iom128 ioa128 iob128 blk128 "
-                                "em592 xa256 xb256"),
+           "wr": ("sbuf", [128, 4, 128], "bfloat16"), "wi": ("sbuf", [128, 8, 128], "bfloat16")}
+for _d, _names in (("bfloat16", "win4096 idwin4096 pw384 pf16 bs8 idp384 wlb32 halob8 idhi128 idlo128 iom128 ioa128 blk128 "
+                                "shift128 last128 z512 em592 xa256 xb256"),
                    ("int32", "wl32 halo32 wa32 wb32 wd32 we32 wf32 wg32 wh32 wj32 wq32 tidr128 ta128 tz128 tl128 pgi1 iop1 ri1 "
                              "wsi1 keyi32 leni32 idi32"),
-                   ("float32", "lp24 ctmp16 cnext1 pg1 iof16 rr1 ws1 rm16 eq8 dd4 da4 db4 ca1 cb1 lowr1 ea1 eb1 bc1 bk6 "
-                               "zer32 dk128 dz64 dy320 sca64 scb64 scy320 scz128 best32 yl32 yi32"),
+                   ("float32", "lp24 pg1 iof16 rr1 ws1 rm16 eq8 dd4 da4 db4 ca1 cb1 lowr1 ea1 eb1 bc1 bk6 "
+                               "zer32 dk128 dz64 dy192 dv128 sca64 scb64 scy192 scv128 scz128 top32 best32 yl32 yi32"),
                    ("uint16", "lone2 ltwo2 lpre24 lc32 lq32")):
     for _n in _names.split():
         _b = _n.rstrip("0123456789")
@@ -20,7 +19,7 @@ for _k in range(1, 7):
     if _k > 2:
         SCRATCH["l%d" % _k] = ("sbuf", [128, 32], "uint16")
     SCRATCH["y%d" % _k] = ("sbuf", [128, 512], "bfloat16")
-for _k in (0, 1, 2, 4, 5):
+for _k in range(6):
     SCRATCH["p%d" % _k] = ("psum", [128, 512], "float32")
 SEMAPHORES = ["cv", "cs", "ct", "cg", "dl", "dr", "dt", "dhi", "dlo", "drr", "didw", "dyl", "dyi"] + \
              [a + b for a in ("r", "id", "x", "p", "n", "k") for b in ("_in", "_out")] + ["dk%d" % k for k in range(4)]
@@ -82,33 +81,33 @@ def rank_program(g, core, T, topo):
     lett_ld = done("dl", sy.dma_start(T.wl[:], T.lett[:]), 16)
 
     ip = G(g.iota(T.iop[:], [[0, 1]], 0, 1))
-    G(g.iota(T.iom[:], [[16, 8], [0, 16]], 0, 0, allow_small_or_imprecise_dtypes=True))
+    io = G(g.iota(T.iom[:], [[16, 8], [0, 16]], 0, 0, allow_small_or_imprecise_dtypes=True))
     iof = G(g.iota(T.iof[:], [[1, 16]], 0, 0, allow_small_or_imprecise_dtypes=True))
+    bs = G(g.iota(T.bs[:], [[512, 8]], 256, 0, allow_small_or_imprecise_dtypes=True))
+    idz = V(v.memset(T.idwin[:, 0:512], 0.0))
     hz = V(v.memset(T.halo[:], 0))
     V(v.memset(T.pw[:, pb0 + 32:pb0 + NB], 0.0))
     wait("v", ip)
     V(v.tensor_scalar(T.pgi[:], T.iop[:], 112, None, A.bitwise_and))
     k0 = V(v.tensor_scalar(T.ri[:], T.iop[:], 15, None, A.bitwise_and))
-    idz = V(v.memset(T.idwin[:, 0:1024], 0.0))
+    V(v.memset(T.eq[:], 1.0))
     wait("v", k0)
-    V(v.tensor_copy(T.pg[:], T.pgi[:]))
+    kp = V(v.tensor_copy(T.pg[:], T.pgi[:]))
     k1 = V(v.tensor_copy(T.rr[:], T.ri[:]))
     k2 = V(v.tensor_scalar(T.wsi[:], T.ri[:], 2, None, A.arith_shift_right))
-    V(v.memset(T.zer[:], 0.0))
-    wait("v", k1, iof)
+    wait("v", io, kp)
     bl = V(v.tensor_scalar(T.blk[:], T.iom[:], T.pg[:, 0:1], None, A.is_equal))
+    wait("v", k1, iof)
     rm = V(v.tensor_scalar(T.rm[:], T.iof[:], T.rr[:, 0:1], None, A.is_equal))
 
     wait("v", tid_ld)
     V(v.tensor_scalar(T.ta[0:32, :], T.tidr[0:32, :], 65280, None, A.bitwise_and))
     a3 = V(v.tensor_scalar(T.tz[0:32, :], T.tidr[0:32, :], 0, -524288, A.is_equal, A.mult))
     a4 = V(v.tensor_scalar(T.tl[0:32, :], T.tidr[0:32, :], 255, None, A.bitwise_and))
-    k3 = V(v.tensor_scalar(T.bc[:], T.rr[:], 2.0, 65536.0, A.is_equal, A.mult))
     wait("v", a3)
     hi = V(v.tensor_tensor(T.idhi[0:32, :], T.ta[0:32, :], T.tz[0:32, :], A.add))
     wait("v", a4)
     lo = V(v.tensor_copy(T.idlo[0:32, :], T.tl[0:32, :]))
-    V(v.memset(T.eq[:], 1.0))
     wait("y", hi)
     hi_st = done("dhi", sy.dma_start(T.idl[me, 0:64, :], T.idhi[0:32, :]), 16)
     wait("y", lo)
@@ -117,16 +116,12 @@ def rank_program(g, core, T, topo):
     wait("g", r_own)
     r_in = send(T.rl[me], "r", [T.cores[(me - 1) % N]])
     io4 = G(g.iota(T.ioa[:], [[16, 8], [0, 4], [1, 4]], 0, 0, allow_small_or_imprecise_dtypes=True))
-    io8 = G(g.iota(T.iob[:], [[16, 8], [0, 2], [1, 8]], 0, 0, allow_small_or_imprecise_dtypes=True))
-    bs = G(g.iota(T.bs[:], [[512, 8]], 256, 0, allow_small_or_imprecise_dtypes=True))
     wait("g", hi_st, lo_st)
     id_in = send(T.idl[me], "id", peers)
 
-    wait("s", rm, bl)
-    for r in range(16):
-        pk = S(s.activation(T.pick[:, r, :], T.blk[:], F.Copy, scale=T.rm[:, r:r + 1]))
     wait("s", idz)
-    for n in (1024, 2048):
+    S(s.activation(T.zer[:], T.idwin[:, 0:32], F.Copy))
+    for n in (512, 1024, 2048):
         idz = S(s.activation(T.idwin[:, n:2 * n], T.idwin[:, 0:n], F.Copy))
         wait("s", idz)
 
@@ -135,9 +130,10 @@ def rank_program(g, core, T, topo):
         wait("v", kid_ld[j])
         kc = V(v.tensor_scalar(T.kb[:, :, 32 * a + 16 * gl:32 * a + 16 * gl + 16],
                                T.kraw[:, 16 * gl + 8 * a:16 * gl + 8 * a + 8, :], 256, None, A.subtract))
-    wait("v", k2, k3)
-    k4 = V(v.tensor_copy(T.ws[:], T.wsi[:]))
-    V(v.tensor_scalar(T.bk[:], T.iof[:, 1:7], T.bc[:, 0:1], None, A.mult))
+        if j == 1:
+            k3 = V(v.tensor_scalar(T.bc[:], T.rr[:], 2.0, 65536.0, A.is_equal, A.mult))
+            wait("v", k2)
+            k4 = V(v.tensor_copy(T.ws[:], T.wsi[:]))
     wait("v", kc)
     for m in (1, 0, 2, 3, 4, 5, 6, 7):
         ev = V(v.transpose(T.win[:, wb0 + m:wb0 + 512:8], T.kb[:, m, :]))
@@ -146,90 +142,105 @@ def rank_program(g, core, T, topo):
         if m == 6:
             wait("v", root)
             l1 = V(v.tensor_scalar(T.lone[:, 0:1], T.win[:, wb0 + 1:wb0 + 2], 256, None, A.add))
-            V(v.tensor_copy(T.pw[:, pb0 + 34:pb0 + 35], T.win[:, wb0 + 1:wb0 + 2]))
     wait("g", ev)
     x_in = send(T.win[:, wb0:wb0 + 512], "x", [partner])
 
     wait("v", ev, l1)
     g1 = V(v.tensor_copy(T.pf[:], T.win[:, wb0:wb0 + 512].indirect(T.lone[:, 0:1])))
-    wait("v", k4, lett_ld)
-    wb = V(v.tensor_copy(T.wlb[:], T.wl[:]))
+    V(v.tensor_copy(T.pw[:, pb0 + 34:pb0 + 35], T.win[:, wb0 + 1:wb0 + 2]))
     wait("v", g1)
     l2 = V(v.tensor_scalar(T.ltwo[:], T.pf[:, 2 * me:2 * me + 2], 256, None, A.add))
     V(v.tensor_copy(T.pw[:, pb0 + 32:pb0 + 34], T.pf[:, 2 * me:2 * me + 2]))
     wait("v", l2)
     p3 = V(v.tensor_copy(T.pw[:, pb0:pb0 + 32], T.win[:, wb0:wb0 + 512].indirect(T.ltwo[:])))
+    wait("v", k4, lett_ld)
+    wb = V(v.tensor_copy(T.wlb[:], T.wl[:]))
     wait("g", p3)
     p_in = send(T.pw[:, pb0:pb0 + NB], "p", [partner])
+    wait("g", bl)
+    G(g.affine_select(T.shift[:], T.blk[:], [[1, 128]], A.is_equal, 0.0, 1, -1))
+    sh = G(g.affine_select(T.last[:], T.blk[:], [[1, 128]], A.is_equal, 0.0, -15, -1))
     wait("g", p_in)
     n_in = send(T.pw[:, 2 * NB * at:2 * NB * at + 2 * NB], "n", near)
     wait("g", x_in)
     k_in = send(T.win[:, 1024 * at:1024 * at + 1024], "k", near)
+    for i in range(8):
+        wi = G(g.affine_select(T.wi[:, i, :], T.blk[:], [[0, 16], [1, 8]], A.is_equal, 0.0, -i, 0))
     wait("y", r_in, hz)
     rr_ld = done("drr", sy.dma_start(T.halo[0:128:16, :], T.rl[(me + 1) % N]), 16)
 
-    wait("t", pk, wb)
+    wait("s", wb, rm)
     for r in range(16):
-        P(t.matmul(T.p4[:, r::16], T.pick[:, r, :], T.wlb[:], True, True))
-    for r in range(15):
-        P(t.matmul(T.p5[:, r:80:16], T.pick[:, r + 1, :], T.wlb[:, 0:5], True, True))
+        zs = S(s.activation(T.z[:, r::16], T.wlb[:], F.Copy, scale=T.rm[:, r:r + 1]))
+    c1 = V(v.tensor_scalar(T.eq[:, 0:4], T.iof[:, 0:4], T.ws[:, 0:1], None, A.is_equal))
     V(v.tensor_scalar(T.wa[:], T.wl[:], 6, None, A.bitwise_and))
     c2 = V(v.tensor_scalar(T.wb[:], T.wl[:], 3, None, A.arith_shift_right))
-    c5 = V(v.tensor_scalar(T.wd[:], T.wl[:], 1, None, A.bitwise_and))
-    c1 = V(v.tensor_scalar(T.eq[:, 0:4], T.iof[:, 0:4], T.ws[:, 0:1], None, A.is_equal))
-    wait("v", c2)
-    c2 = V(v.tensor_tensor(T.wq[:], T.wa[:], T.wb[:], A.add))
     wait("v", c1)
     c3 = V(v.tensor_tensor(T.dd[:], T.eq[:, 0:4], T.eq[:, 1:5], A.subtract))
-    c5 = V(v.tensor_scalar(T.we[:], T.wd[:], 16, None, A.mult))
-    wait("v", c3)
-    V(v.tensor_scalar(T.da[:], T.dd[:], 16384.0, None, A.mult))
-    c4 = V(v.tensor_scalar(T.ca[:], T.dd[:, 3:4], 16384.0, 7936.0, A.mult, A.subtract))
-    wait("v", c2, c5)
-    c7 = V(v.tensor_scalar(T.wf[:], T.wq[:], NB, None, A.mult))
-    V(v.tensor_tensor(T.wg[:, 0:31], T.we[:, 0:31], T.wl[:, 1:32], A.add))
+    low = V(v.tensor_scalar(T.lowr[:], T.ws[:], 2.0, None, A.is_lt))
+    c5 = V(v.tensor_scalar(T.wd[:], T.wl[:], 1, None, A.bitwise_and))
+    wait("v", c2)
+    c2 = V(v.tensor_tensor(T.wq[:], T.wa[:], T.wb[:], A.add))
     wait("v", rr_ld)
     hb = V(v.tensor_copy(T.halob[:], T.halo[:, 0:8]))
-    wait("t", hb)
-    ex = P(t.matmul(T.p5[:, 15:80:16], T.pick[:, 0, :], T.halob[:, 0:5], True, True))
+    wait("v", c5)
+    c5 = V(v.tensor_scalar(T.we[:], T.wd[:], 16, None, A.mult))
+    wait("v", c2)
+    c7 = V(v.tensor_scalar(T.wf[:], T.wq[:], NB, None, A.mult))
+    wait("v", c5)
+    V(v.tensor_tensor(T.wg[:, 0:31], T.we[:, 0:31], T.wl[:, 1:32], A.add))
     wait("v", c7)
     c7 = V(v.tensor_tensor(T.wj[:], T.wf[:], T.wl[:], A.add))
+    wait("t", wb, hb, bl, sh)
+    P(t.matmul(T.p3[:, 0:1], T.shift[:], T.wlb[:, 0:1], True, False))
+    cn = P(t.matmul(T.p3[:, 0:1], T.last[:], T.halob[:, 0:1], False, True))
+    P(t.matmul(T.p5[:, 0:5], T.blk[:], T.halob[:, 0:5], True, True))
+    wait("t", zs)
+    el = P(t.matmul(T.p4[:], T.blk[:], T.z[:], True, True))
     wait("v", io4)
     for i in range(4):
         V(v.tensor_scalar(T.wr[:, i, :], T.ioa[:], float(-i), T.pg[:, 0:1], A.add, A.is_equal))
-    wait("v", c4)
-    for w in range(3):
-        V(v.tensor_scalar(T.dk[:, w::4], T.zer[:], T.da[:, w:w + 1], None, A.add))
     wait("v", c7)
     V(v.tensor_copy(T.lc[:], T.wj[:]))
-    dcon = V(v.tensor_scalar(T.dk[:, 3::4], T.wq[:], 512.0, T.ca[:, 0:1], A.mult, A.add))
-    wait("v", ex)
-    c6 = V(v.tensor_tensor(T.ctmp[:], T.p5[:, 0:16], T.rm[:], A.mult))
-    V(v.tensor_scalar(T.em[:, 512:592], T.p5[:, 0:80], T.rr[:, 0:1], None, A.is_equal))
-    wait("v", c6)
-    c6 = V(v.tensor_reduce(T.cnext[:], T.ctmp[:], AxisListType.X, A.add))
-    V(v.tensor_scalar(T.em[:, 0:512], T.p4[:], T.rr[:, 0:1], None, A.is_equal))
-    wait("v", c6, io8)
-
-    def id_weight(i):
-        return V(v.tensor_scalar(T.wi[:, i, :], T.iob[:], float(-i), T.pg[:, 0:1], A.add, A.is_equal))
-    c6 = V(v.tensor_scalar(T.wg[:, 31:32], T.we[:, 31:32], T.cnext[:, 0:1], None, A.add))
-    id_weight(0)
+    wait("v", cn)
+    c6 = V(v.tensor_scalar(T.wg[:, 31:32], T.we[:, 31:32], T.p3[:, 0:1], None, A.add))
+    wait("v", el)
+    em = V(v.tensor_scalar(T.em[:, 512:591], T.p4[:, 1:80], T.rr[:, 0:1], None, A.is_equal))
     wait("v", c6)
     c6 = V(v.tensor_tensor(T.wh[:], T.wf[:], T.wg[:], A.add))
-    id_weight(1)
-    wait("v", c6)
+    V(v.tensor_scalar(T.em[:, 0:512], T.p4[:], T.rr[:, 0:1], None, A.is_equal))
+    wait("v", em, c6)
     lq = V(v.tensor_copy(T.lq[:], T.wh[:]))
-    for i in range(2, 8):
-        wi = id_weight(i)
+    em = V(v.tensor_scalar(T.em[:, 527:592:16], T.p5[:, 0:5], T.rr[:, 0:1], None, A.is_equal))
+
+    wait("s", c3, low, k3, iof)
+    S(s.activation(T.da[:], T.dd[:], F.Identity, scale=16384.0))
+    c4 = S(s.activation(T.ca[:], T.dd[:, 3:4], F.Identity, bias=-7936.0, scale=16384.0))
+    S(s.activation(T.db[:], T.dd[:], F.Identity, scale=1048576.0))
+    S(s.activation(T.cb[:], T.dd[:, 3:4], F.Identity, bias=-2097152.0, scale=1048576.0))
+    S(s.activation(T.ea[:], T.lowr[:], F.Identity, bias=-1048576.0, scale=2097152.0))
+    c8 = S(s.activation(T.eb[:], T.lowr[:], F.Identity, bias=-2097152.0, scale=-1048576.0))
+    S(s.activation(T.bk[:], T.iof[:, 1:7], F.Copy, scale=T.bc[:, 0:1]))
+    wait("s", c4)
+    for w in range(3):
+        c9 = S(s.activation(T.dk[:, w::4], T.zer[:], F.Identity, bias=T.da[:, w:w + 1]))
 
     wait("y", id_in, hi_st, lo_st, idz)
-    wait("s", id_in, hi_st, lo_st, idz)
     for j in range(N):
         b = 512 * pos[j]
         done("didw", sy.dma_start(T.idwin[0:128:16, b:b + 512], T.idl[j, 0:64, :]), 16)
-        done("didw", s.dma_start(T.idwin[1:128:16, b:b + 512], T.idl[j, 64:128, :]), 16)
+        done("didw", sy.dma_start(T.idwin[1:128:16, b:b + 512], T.idl[j, 64:128, :]), 16)
     idw = ("didw", total["didw"])
+
+    wait("s", c8)
+    for w in range(4):
+        S(s.activation(T.dz[:, w::4], T.zer[:, 0:16], F.Identity, bias=T.db[:, w:w + 1] if w < 3 else T.cb[:, 0:1]))
+    for d, n in ((T.dy, 3), (T.dv, 2)):
+        for w in range(2 * n):
+            if w in (n - 1, 2 * n - 1):
+                cy = S(s.activation(d[:, w::2 * n], T.zer[:], F.Identity, bias=(T.ea if w == n - 1 else T.eb)[:, 0:1]))
+            else:
+                cy = S(s.activation(d[:, w::2 * n], T.zer[:], F.Copy))
     X = [T.xa, T.xb]
     SC = [T.sca, T.scb]
 
@@ -241,16 +252,16 @@ def rank_program(g, core, T, topo):
 
     yt, ys, lt, sc, xt, ks = {}, {}, {}, {}, {}, {}
 
-    def id_sum(k, part):
+    def id_sum(k):
         wait("t", yt[k, 0], yt[k, 1], wi)
-        for i in range(4 * part, 4 * part + 4):
-            ys[k] = P(t.matmul(T.p2[:, k - 1:320:5], T.wi[:, i, :], T["y%d" % k][:, i::8], i == 0, i == 7))
+        out = T.p2[:, k - 1:192:3] if k < 4 else T.p3[:, k - 4:128:2]
+        for i in range(8):
+            ys[k] = P(t.matmul(out, T.wi[:, i, :], T["y%d" % k][:, i::8], i == 0, i == 7))
 
-    sums = {(3, 0): [(1, 0)], (3, 1): [(1, 1)], (4, 0): [(2, 0)], (4, 1): [(2, 1)], (5, 0): [(3, 0)],
-            (5, 1): [(3, 1), (4, 0), (4, 1)], (6, 0): [(5, 0), (5, 1)]}
+    sums = {(3, 1): [1], (4, 1): [2, 3], (5, 1): [4], (6, 0): [5]}
 
     def scan(k, h):
-        wait("v", ks[h], dcon)
+        wait("v", ks[h], dcon, c9)
         sc[h] = V(v.tensor_tensor_scan(SC[h][:], T["p%d" % h][:, 0:64], T.dk[:, 64 * h:64 * h + 64], -8192.0, A.max, A.add))
 
     def node_list(k, h):
@@ -271,20 +282,23 @@ def rank_program(g, core, T, topo):
         else:
             wait("v", lt[h], idw)
             yt[k, h] = V(v.tensor_scalar(y, T.idwin[:].indirect(off), bias, None, A.add))
-        for a, b in sums.get((k, h), []):
-            id_sum(a, b)
+        for a in sums.get((k, h), []):
+            id_sum(a)
 
     for h in range(2):
-        wait("v", lq, p3, p_in, n_in)
+        wait("v", em, lq, p3, p_in, n_in)
         xt[h] = V(v.tensor_tensor(X[h][:], T.pw[:].indirect(T.lq[:, 16 * h:16 * h + 16]),
                                   T.em[:, 16 * (2 + 16 * h):16 * (2 + 16 * h) + 256], A.mult))
         ks[h] = kid_sum(h, xt[h])
-    wait("v", bs)
-    for i in range(3):
-        b = V(v.tensor_tensor(T.lp[:, i::3], T.pw[:, 32 + i::NB], T.bs[:], A.add))
-    wait("v", b)
-    lp = V(v.tensor_copy(T.lpre[:], T.lp[:]))
-    wait("s", lp, idw)
+        if h == 0:
+            wait("v", bs)
+            for i in range(3):
+                b = V(v.tensor_tensor(T.lp[:, i::3], T.pw[:, 32 + i::NB], T.bs[:], A.add))
+            wait("v", c4)
+            dcon = V(v.tensor_scalar(T.dk[:, 3::4], T.wq[:], 512.0, T.ca[:, 0:1], A.mult, A.add))
+            wait("v", b)
+            lp = V(v.tensor_copy(T.lpre[:], T.lp[:]))
+    wait("s", lp, idw, cy)
     idp = S(s.activation(T.idp[:], T.idwin[:].indirect(T.lpre[:]), F.Copy))
     wait("s", idp)
     for h in range(2):
@@ -294,42 +308,30 @@ def rank_program(g, core, T, topo):
         yt[2, h] = S(s.activation(T.y2[:, 256 * h:256 * h + 256], T.idp[:].indirect(T.lq[:, 16 * h:16 * h + 16]),
                                   F.Identity, bias=T.bk[:, 1:2]))
 
-    def gap(k):
-        if k == 3:
-            V(v.tensor_scalar(T.db[:], T.dd[:], 1048576.0, None, A.mult))
-            V(v.tensor_scalar(T.cb[:], T.dd[:, 3:4], 1048576.0, 2097152.0, A.mult, A.subtract))
-            return V(v.tensor_scalar(T.lowr[:], T.ws[:], 2.0, None, A.is_lt))
-        if k == 4:
-            V(v.tensor_scalar(T.ea[:], T.lowr[:], 2097152.0, 1048576.0, A.mult, A.subtract))
-            V(v.tensor_scalar(T.eb[:], T.lowr[:], -1048576.0, 2097152.0, A.mult, A.subtract))
-            return V(v.memset(T.dy[:], 0.0))
-        if k == 5:
-            for w in range(4):
-                V(v.tensor_scalar(T.dz[:, w::4], T.zer[:, 0:16], T.db[:, w:w + 1] if w < 3 else T.cb[:, 0:1], None, A.add))
-        if k == 6:
-            V(v.tensor_scalar(T.dy[:, 4::10], T.zer[:], T.ea[:, 0:1], None, A.add))
-            return V(v.tensor_scalar(T.dy[:, 9::10], T.zer[:], T.eb[:, 0:1], None, A.add))
-
-    made = None
     for k in range(3, 7):
         scan(k, 0)
-        wait("v", made)
-        made = gap(k) or made
+        if k == 6:
+            wait("v", ys[3], cy)
+            b = V(v.tensor_tensor_scan(T.scy[:], T.p2[:, 0:192], T.dy[:], -2097152.0, A.max, A.add))
         scan(k, 1)
-        for f in (node_list, gathers):
-            for h in range(2):
-                f(k, h)
+        for h in range(2):
+            node_list(k, h)
+        if k == 6:
+            wait("v", b)
+            V(v.tensor_scalar(T.top[:], T.scy[:, 5::6], -2097152.0, None, A.max))
+        for h in range(2):
+            gathers(k, h)
     for h in range(2):
         wait("t", yt[6, h])
         for i in range(4):
             ys[6, h] = P(t.matmul(T["p%d" % (4 + h)][:, 0:64], T.wr[:, i, :], T.y6[:, 256 * h + i:256 * h + 256:4], i == 0, i == 3))
 
     wait("v", ys[5])
-    a = V(v.tensor_tensor_scan(T.scy[:], T.p2[:, 0:320], T.dy[:], -2097152.0, A.max, A.add))
+    a = V(v.tensor_tensor_scan(T.scv[:], T.p3[:, 0:128], T.dv[:], -2097152.0, A.max, A.add))
     wait("v", ys[6, 0])
     V(v.tensor_tensor_scan(T.scz[:, 0:64], T.p4[:, 0:64], T.dz[:], -2097152.0, A.max, A.add))
     wait("v", a)
-    V(v.tensor_scalar(T.best[:], T.scy[:, 9::10], -2097152.0, None, A.max))
+    V(v.tensor_tensor(T.best[:], T.top[:], T.scv[:, 3::4], A.max))
     wait("v", ys[6, 1])
     a = V(v.tensor_tensor_scan(T.scz[:, 64:128], T.p5[:, 0:64], T.dz[:], -2097152.0, A.max, A.add))
     wait("v", a)

from concourse.bass import DstId, RemoteDMATransfer
from concourse.mybir import AluOpType as A, ActivationFunctionType as F

N = 8
SCRATCH = {"rl": ("dram", [8, 128, 2], "int32"), "idl": ("dram", [8, 128, 64], "bfloat16"),
           "kraw": ("sbuf", [128, 32, 16], "int32"), "kb": ("sbuf", [128, 8, 64], "bfloat16"),
           "wr": ("sbuf", [128, 4, 128], "bfloat16"), "wi": ("sbuf", [128, 8, 128], "bfloat16")}
for _d, _names in (("bfloat16", "win4096 idwin4096 pw384 pf16 bs8 idp384 wlb32 halob8 idhi128 idlo128 iom128 ioa128 blk128 "
                                "shift128 last128 z512 em592 xa256 xb256"),
                   ("int32", "wl32 halo32 wa32 wb32 wd32 we32 wf32 wg32 wh32 wj32 wq32 tidr128 ta128 tz128 tl128 pgi1 iop1 ri1 "
                             "wsi1 keyi32 leni32 idi32"),
                   ("float32", "lp24 pg1 iof16 rr1 ws1 rm16 eq8 dd4 da4 db4 ca1 cb1 lowr1 ea1 eb1 bc1 bk6 "
                               "zer32 dk128 dz64 dy192 dv128 sca64 scb64 scy192 scv128 scz128 top32 best32 yl32 yi32"),
                   ("uint16", "lone2 ltwo2 lpre24 lc32 lq32")):
    for _n in _names.split():
        _b = _n.rstrip("0123456789")
        SCRATCH[_b] = ("sbuf", [128, int(_n[len(_b):])], _d)
for _k in range(1, 7):
    if _k > 2:
        SCRATCH["l%d" % _k] = ("sbuf", [128, 32], "uint16")
    SCRATCH["y%d" % _k] = ("sbuf", [128, 512], "bfloat16")
for _k in range(6):
    SCRATCH["p%d" % _k] = ("psum", [128, 512], "float32")
SEMAPHORES = ["cv", "cs", "ct", "cg", "dl", "dr", "dt", "dhi", "dlo", "drr", "didw", "dyl", "dyi"] + \
             [a + b for a in ("r", "id", "x", "p", "n", "k") for b in ("_in", "_out")] + ["dk%d" % k for k in range(4)]


def rank_program(g, core, T, topo):
    me = T.rank_of(core)
    if me is None:
        return
    q = {"v": g.vector, "s": g.scalar, "t": g.tensor, "g": g, "y": g.sync}
    total, seen = {}, {k: {} for k in q}

    def wait(k, *toks):
        for tok in toks:
            if tok is not None and seen[k].get(tok[0], 0) < tok[1]:
                q[k].wait_ge(T.sem[tok[0]], tok[1])
                seen[k][tok[0]] = tok[1]

    def done(sem, inst, n=1):
        inst.then_inc(T.sem[sem], n)
        total[sem] = total.get(sem, 0) + n
        return (sem, total[sem])

    def V(inst): return done("cv", inst)
    def S(inst): return done("cs", inst)
    def P(inst): return done("ct", inst)
    def G(inst): return done("cg", inst)
    v, s, t, sy = g.vector, g.scalar, g.tensor, g.sync
    H, NB = N // 2, 48
    peers = [T.cores[(me + d) % N] for d in range(1, N)]
    pos = [2 * (j % H) + j // H for j in range(N)]
    at, partner = me % H, T.cores[(me + H) % N]
    near = [T.cores[me - at + (at + d) % H] for d in range(1, H)]
    wb0, pb0 = 512 * pos[me], NB * pos[me]

    def dst(c):
        a = topo.addr(c)
        return DstId(rid=a[0], pnc=a[1])

    def send(src, name, to):
        mask = topo.mask(core, to[0])
        for c in to:
            mask = mask & topo.mask(core, c)
        ne = bin(mask).count("1")
        g.remote_dma_fused([RemoteDMATransfer(dst_ids=[dst(c) for c in to], dma_engine_mask=mask,
                                              remote_sem=T.sem[name + "_in"], srcs=[src], dsts=[src for c in to])],
                           local_sem=T.sem[name + "_out"])
        total[name + "_out"] = ne
        total[name + "_in"] = ne * len(to)
        return (name + "_in", ne * len(to))

    r_own = done("dr", sy.dma_start(T.rl[me], T.lett[:, 0:32]), 16)
    tid_ld = done("dt", s.dma_start(T.tidr[0:32, :], T.tid[:]), 16)
    kid_ld = []
    for j in range(4):
        a, gl = j // 2, j % 2
        kid_ld.append(done("dk%d" % j, (sy, s)[gl].dma_start(T.kraw[:, 16 * gl + 8 * a:16 * gl + 8 * a + 8, :],
                                                             T.kid[gl::2, 4096 * a:4096 * a + 4096]), 16))
    lett_ld = done("dl", sy.dma_start(T.wl[:], T.lett[:]), 16)

    ip = G(g.iota(T.iop[:], [[0, 1]], 0, 1))
    io = G(g.iota(T.iom[:], [[16, 8], [0, 16]], 0, 0, allow_small_or_imprecise_dtypes=True))
    iof = G(g.iota(T.iof[:], [[1, 16]], 0, 0, allow_small_or_imprecise_dtypes=True))
    bs = G(g.iota(T.bs[:], [[512, 8]], 256, 0, allow_small_or_imprecise_dtypes=True))
    idz = V(v.memset(T.idwin[:, 0:512], 0.0))
    hz = V(v.memset(T.halo[:], 0))
    V(v.memset(T.pw[:, pb0 + 32:pb0 + NB], 0.0))
    wait("v", ip)
    V(v.tensor_scalar(T.pgi[:], T.iop[:], 112, None, A.bitwise_and))
    k0 = V(v.tensor_scalar(T.ri[:], T.iop[:], 15, None, A.bitwise_and))
    V(v.memset(T.eq[:], 1.0))
    wait("v", k0)
    kp = V(v.tensor_copy(T.pg[:], T.pgi[:]))
    k1 = V(v.tensor_copy(T.rr[:], T.ri[:]))
    k2 = V(v.tensor_scalar(T.wsi[:], T.ri[:], 2, None, A.arith_shift_right))
    wait("v", io, kp)
    bl = V(v.tensor_scalar(T.blk[:], T.iom[:], T.pg[:, 0:1], None, A.is_equal))
    wait("v", k1, iof)
    rm = V(v.tensor_scalar(T.rm[:], T.iof[:], T.rr[:, 0:1], None, A.is_equal))

    wait("v", tid_ld)
    V(v.tensor_scalar(T.ta[0:32, :], T.tidr[0:32, :], 65280, None, A.bitwise_and))
    a3 = V(v.tensor_scalar(T.tz[0:32, :], T.tidr[0:32, :], 0, -524288, A.is_equal, A.mult))
    a4 = V(v.tensor_scalar(T.tl[0:32, :], T.tidr[0:32, :], 255, None, A.bitwise_and))
    wait("v", a3)
    hi = V(v.tensor_tensor(T.idhi[0:32, :], T.ta[0:32, :], T.tz[0:32, :], A.add))
    wait("v", a4)
    lo = V(v.tensor_copy(T.idlo[0:32, :], T.tl[0:32, :]))
    wait("y", hi)
    hi_st = done("dhi", sy.dma_start(T.idl[me, 0:64, :], T.idhi[0:32, :]), 16)
    wait("y", lo)
    lo_st = done("dlo", sy.dma_start(T.idl[me, 64:128, :], T.idlo[0:32, :]), 16)

    wait("g", r_own)
    r_in = send(T.rl[me], "r", [T.cores[(me - 1) % N]])
    io4 = G(g.iota(T.ioa[:], [[16, 8], [0, 4], [1, 4]], 0, 0, allow_small_or_imprecise_dtypes=True))
    wait("g", hi_st, lo_st)
    id_in = send(T.idl[me], "id", peers)

    wait("s", idz)
    S(s.activation(T.zer[:], T.idwin[:, 0:32], F.Copy))
    for n in (512, 1024, 2048):
        idz = S(s.activation(T.idwin[:, n:2 * n], T.idwin[:, 0:n], F.Copy))
        wait("s", idz)

    for j in range(4):
        a, gl = j // 2, j % 2
        wait("v", kid_ld[j])
        kc = V(v.tensor_scalar(T.kb[:, :, 32 * a + 16 * gl:32 * a + 16 * gl + 16],
                               T.kraw[:, 16 * gl + 8 * a:16 * gl + 8 * a + 8, :], 256, None, A.subtract))
        if j == 1:
            k3 = V(v.tensor_scalar(T.bc[:], T.rr[:], 2.0, 65536.0, A.is_equal, A.mult))
            wait("v", k2)
            k4 = V(v.tensor_copy(T.ws[:], T.wsi[:]))
    wait("v", kc)
    for m in (1, 0, 2, 3, 4, 5, 6, 7):
        ev = V(v.transpose(T.win[:, wb0 + m:wb0 + 512:8], T.kb[:, m, :]))
        if m == 1:
            root = ev
        if m == 6:
            wait("v", root)
            l1 = V(v.tensor_scalar(T.lone[:, 0:1], T.win[:, wb0 + 1:wb0 + 2], 256, None, A.add))
    wait("g", ev)
    x_in = send(T.win[:, wb0:wb0 + 512], "x", [partner])

    wait("v", ev, l1)
    g1 = V(v.tensor_copy(T.pf[:], T.win[:, wb0:wb0 + 512].indirect(T.lone[:, 0:1])))
    V(v.tensor_copy(T.pw[:, pb0 + 34:pb0 + 35], T.win[:, wb0 + 1:wb0 + 2]))
    wait("v", g1)
    l2 = V(v.tensor_scalar(T.ltwo[:], T.pf[:, 2 * me:2 * me + 2], 256, None, A.add))
    V(v.tensor_copy(T.pw[:, pb0 + 32:pb0 + 34], T.pf[:, 2 * me:2 * me + 2]))
    wait("v", l2)
    p3 = V(v.tensor_copy(T.pw[:, pb0:pb0 + 32], T.win[:, wb0:wb0 + 512].indirect(T.ltwo[:])))
    wait("v", k4, lett_ld)
    wb = V(v.tensor_copy(T.wlb[:], T.wl[:]))
    wait("g", p3)
    p_in = send(T.pw[:, pb0:pb0 + NB], "p", [partner])
    wait("g", bl)
    G(g.affine_select(T.shift[:], T.blk[:], [[1, 128]], A.is_equal, 0.0, 1, -1))
    sh = G(g.affine_select(T.last[:], T.blk[:], [[1, 128]], A.is_equal, 0.0, -15, -1))
    wait("g", p_in)
    n_in = send(T.pw[:, 2 * NB * at:2 * NB * at + 2 * NB], "n", near)
    wait("g", x_in)
    k_in = send(T.win[:, 1024 * at:1024 * at + 1024], "k", near)
    for i in range(8):
        wi = G(g.affine_select(T.wi[:, i, :], T.blk[:], [[0, 16], [1, 8]], A.is_equal, 0.0, -i, 0))
    wait("y", r_in, hz)
    rr_ld = done("drr", sy.dma_start(T.halo[0:128:16, :], T.rl[(me + 1) % N]), 16)

    wait("s", wb, rm)
    for r in range(16):
        zs = S(s.activation(T.z[:, r::16], T.wlb[:], F.Copy, scale=T.rm[:, r:r + 1]))
    c1 = V(v.tensor_scalar(T.eq[:, 0:4], T.iof[:, 0:4], T.ws[:, 0:1], None, A.is_equal))
    V(v.tensor_scalar(T.wa[:], T.wl[:], 6, None, A.bitwise_and))
    c2 = V(v.tensor_scalar(T.wb[:], T.wl[:], 3, None, A.arith_shift_right))
    wait("v", c1)
    c3 = V(v.tensor_tensor(T.dd[:], T.eq[:, 0:4], T.eq[:, 1:5], A.subtract))
    low = V(v.tensor_scalar(T.lowr[:], T.ws[:], 2.0, None, A.is_lt))
    c5 = V(v.tensor_scalar(T.wd[:], T.wl[:], 1, None, A.bitwise_and))
    wait("v", c2)
    c2 = V(v.tensor_tensor(T.wq[:], T.wa[:], T.wb[:], A.add))
    wait("v", rr_ld)
    hb = V(v.tensor_copy(T.halob[:], T.halo[:, 0:8]))
    wait("v", c5)
    c5 = V(v.tensor_scalar(T.we[:], T.wd[:], 16, None, A.mult))
    wait("v", c2)
    c7 = V(v.tensor_scalar(T.wf[:], T.wq[:], NB, None, A.mult))
    wait("v", c5)
    V(v.tensor_tensor(T.wg[:, 0:31], T.we[:, 0:31], T.wl[:, 1:32], A.add))
    wait("v", c7)
    c7 = V(v.tensor_tensor(T.wj[:], T.wf[:], T.wl[:], A.add))
    wait("t", wb, hb, bl, sh)
    P(t.matmul(T.p3[:, 0:1], T.shift[:], T.wlb[:, 0:1], True, False))
    cn = P(t.matmul(T.p3[:, 0:1], T.last[:], T.halob[:, 0:1], False, True))
    P(t.matmul(T.p5[:, 0:5], T.blk[:], T.halob[:, 0:5], True, True))
    wait("t", zs)
    el = P(t.matmul(T.p4[:], T.blk[:], T.z[:], True, True))
    wait("v", io4)
    for i in range(4):
        V(v.tensor_scalar(T.wr[:, i, :], T.ioa[:], float(-i), T.pg[:, 0:1], A.add, A.is_equal))
    wait("v", c7)
    V(v.tensor_copy(T.lc[:], T.wj[:]))
    wait("v", cn)
    c6 = V(v.tensor_scalar(T.wg[:, 31:32], T.we[:, 31:32], T.p3[:, 0:1], None, A.add))
    wait("v", el)
    em = V(v.tensor_scalar(T.em[:, 512:591], T.p4[:, 1:80], T.rr[:, 0:1], None, A.is_equal))
    wait("v", c6)
    c6 = V(v.tensor_tensor(T.wh[:], T.wf[:], T.wg[:], A.add))
    V(v.tensor_scalar(T.em[:, 0:512], T.p4[:], T.rr[:, 0:1], None, A.is_equal))
    wait("v", em, c6)
    lq = V(v.tensor_copy(T.lq[:], T.wh[:]))
    em = V(v.tensor_scalar(T.em[:, 527:592:16], T.p5[:, 0:5], T.rr[:, 0:1], None, A.is_equal))

    wait("s", c3, low, k3, iof)
    S(s.activation(T.da[:], T.dd[:], F.Identity, scale=16384.0))
    c4 = S(s.activation(T.ca[:], T.dd[:, 3:4], F.Identity, bias=-7936.0, scale=16384.0))
    S(s.activation(T.db[:], T.dd[:], F.Identity, scale=1048576.0))
    S(s.activation(T.cb[:], T.dd[:, 3:4], F.Identity, bias=-2097152.0, scale=1048576.0))
    S(s.activation(T.ea[:], T.lowr[:], F.Identity, bias=-1048576.0, scale=2097152.0))
    c8 = S(s.activation(T.eb[:], T.lowr[:], F.Identity, bias=-2097152.0, scale=-1048576.0))
    S(s.activation(T.bk[:], T.iof[:, 1:7], F.Copy, scale=T.bc[:, 0:1]))
    wait("s", c4)
    for w in range(3):
        c9 = S(s.activation(T.dk[:, w::4], T.zer[:], F.Identity, bias=T.da[:, w:w + 1]))

    wait("y", id_in, hi_st, lo_st, idz)
    for j in range(N):
        b = 512 * pos[j]
        done("didw", sy.dma_start(T.idwin[0:128:16, b:b + 512], T.idl[j, 0:64, :]), 16)
        done("didw", sy.dma_start(T.idwin[1:128:16, b:b + 512], T.idl[j, 64:128, :]), 16)
    idw = ("didw", total["didw"])

    wait("s", c8)
    for w in range(4):
        S(s.activation(T.dz[:, w::4], T.zer[:, 0:16], F.Identity, bias=T.db[:, w:w + 1] if w < 3 else T.cb[:, 0:1]))
    for d, n in ((T.dy, 3), (T.dv, 2)):
        for w in range(2 * n):
            if w in (n - 1, 2 * n - 1):
                cy = S(s.activation(d[:, w::2 * n], T.zer[:], F.Identity, bias=(T.ea if w == n - 1 else T.eb)[:, 0:1]))
            else:
                cy = S(s.activation(d[:, w::2 * n], T.zer[:], F.Copy))
    X = [T.xa, T.xb]
    SC = [T.sca, T.scb]

    def kid_sum(h, tok):
        wait("t", tok)
        for i in range(4):
            r = P(t.matmul(T["p%d" % h][:, 0:64], T.wr[:, i, :], X[h][:, i::4], i == 0, i == 3))
        return r

    yt, ys, lt, sc, xt, ks = {}, {}, {}, {}, {}, {}

    def id_sum(k):
        wait("t", yt[k, 0], yt[k, 1], wi)
        out = T.p2[:, k - 1:192:3] if k < 4 else T.p3[:, k - 4:128:2]
        for i in range(8):
            ys[k] = P(t.matmul(out, T.wi[:, i, :], T["y%d" % k][:, i::8], i == 0, i == 7))

    sums = {(3, 1): [1], (4, 1): [2, 3], (5, 1): [4], (6, 0): [5]}

    def scan(k, h):
        wait("v", ks[h], dcon, c9)
        sc[h] = V(v.tensor_tensor_scan(SC[h][:], T["p%d" % h][:, 0:64], T.dk[:, 64 * h:64 * h + 64], -8192.0, A.max, A.add))

    def node_list(k, h):
        wait("v", sc[h])
        lt[h] = V(v.tensor_scalar(T["l%d" % k][:, 16 * h:16 * h + 16], SC[h][:, 3::4], 8192.0, None, A.add))

    def gathers(k, h):
        off = T["l%d" % k][:, 16 * h:16 * h + 16]
        y, bias = T["y%d" % k][:, 256 * h:256 * h + 256], T.bk[:, k - 1:k]
        if k < 6:
            wait("v", lt[h], x_in, k_in, ev)
            xt[h] = V(v.tensor_tensor(X[h][:], T.win[:].indirect(off), T.em[:, 16 * (k + 16 * h):16 * (k + 16 * h) + 256],
                                      A.mult))
            ks[h] = kid_sum(h, xt[h])
        if k < 6 or h == 0:
            wait("s", lt[h], idw)
            yt[k, h] = S(s.activation(y, T.idwin[:].indirect(off), F.Identity, bias=bias))
        else:
            wait("v", lt[h], idw)
            yt[k, h] = V(v.tensor_scalar(y, T.idwin[:].indirect(off), bias, None, A.add))
        for a in sums.get((k, h), []):
            id_sum(a)

    for h in range(2):
        wait("v", em, lq, p3, p_in, n_in)
        xt[h] = V(v.tensor_tensor(X[h][:], T.pw[:].indirect(T.lq[:, 16 * h:16 * h + 16]),
                                  T.em[:, 16 * (2 + 16 * h):16 * (2 + 16 * h) + 256], A.mult))
        ks[h] = kid_sum(h, xt[h])
        if h == 0:
            wait("v", bs)
            for i in range(3):
                b = V(v.tensor_tensor(T.lp[:, i::3], T.pw[:, 32 + i::NB], T.bs[:], A.add))
            wait("v", c4)
            dcon = V(v.tensor_scalar(T.dk[:, 3::4], T.wq[:], 512.0, T.ca[:, 0:1], A.mult, A.add))
            wait("v", b)
            lp = V(v.tensor_copy(T.lpre[:], T.lp[:]))
    wait("s", lp, idw, cy)
    idp = S(s.activation(T.idp[:], T.idwin[:].indirect(T.lpre[:]), F.Copy))
    wait("s", idp)
    for h in range(2):
        yt[1, h] = S(s.activation(T.y1[:, 256 * h:256 * h + 256], T.idp[:, 32:384].indirect(T.lc[:, 16 * h:16 * h + 16]),
                                  F.Identity, bias=T.bk[:, 0:1]))
    for h in range(2):
        yt[2, h] = S(s.activation(T.y2[:, 256 * h:256 * h + 256], T.idp[:].indirect(T.lq[:, 16 * h:16 * h + 16]),
                                  F.Identity, bias=T.bk[:, 1:2]))

    for k in range(3, 7):
        scan(k, 0)
        if k == 6:
            wait("v", ys[3], cy)
            b = V(v.tensor_tensor_scan(T.scy[:], T.p2[:, 0:192], T.dy[:], -2097152.0, A.max, A.add))
        scan(k, 1)
        for h in range(2):
            node_list(k, h)
        if k == 6:
            wait("v", b)
            V(v.tensor_scalar(T.top[:], T.scy[:, 5::6], -2097152.0, None, A.max))
        for h in range(2):
            gathers(k, h)
    for h in range(2):
        wait("t", yt[6, h])
        for i in range(4):
            ys[6, h] = P(t.matmul(T["p%d" % (4 + h)][:, 0:64], T.wr[:, i, :], T.y6[:, 256 * h + i:256 * h + 256:4], i == 0, i == 3))

    wait("v", ys[5])
    a = V(v.tensor_tensor_scan(T.scv[:], T.p3[:, 0:128], T.dv[:], -2097152.0, A.max, A.add))
    wait("v", ys[6, 0])
    V(v.tensor_tensor_scan(T.scz[:, 0:64], T.p4[:, 0:64], T.dz[:], -2097152.0, A.max, A.add))
    wait("v", a)
    V(v.tensor_tensor(T.best[:], T.top[:], T.scv[:, 3::4], A.max))
    wait("v", ys[6, 1])
    a = V(v.tensor_tensor_scan(T.scz[:, 64:128], T.p5[:, 0:64], T.dz[:], -2097152.0, A.max, A.add))
    wait("v", a)
    a = V(v.tensor_tensor(T.keyi[:], T.best[:], T.scz[:, 3::4], A.max))
    wait("v", a)
    a = V(v.tensor_scalar(T.leni[:], T.keyi[:], 16, None, A.arith_shift_right))
    b = V(v.tensor_scalar(T.idi[:], T.keyi[:], 65535, None, A.bitwise_and))
    wait("v", a)
    a = V(v.tensor_scalar(T.yl[:], T.leni[:], 32, None, A.add))
    wait("v", b)
    b = V(v.tensor_copy(T.yi[:], T.idi[:]))
    wait("y", a)
    done("dyl", sy.dma_start(T.ylen[:], T.yl[:]), 16)
    wait("s", b)
    done("dyi", s.dma_start(T.yid[:], T.yi[:]), 16)
    for name in SEMAPHORES:
        wait("g", (name, total[name]))
